import numpy as np
import ml_dtypes


def mxq(x, axis, fmt="e4m3"):
    dtype, down = {"e4m3": (ml_dtypes.float8_e4m3fn, 7), "e5m2": (ml_dtypes.float8_e5m2, 14)}[fmt]
    v = np.moveaxis(np.asarray(x, np.float32).astype(ml_dtypes.bfloat16).astype(np.float64), axis, -1)
    blocks = v.reshape(v.shape[:-1] + (-1, 32))
    amax = np.abs(blocks).max(-1, keepdims=True)
    byte = np.maximum(np.where(amax > 0, np.frexp(amax)[1] - 1 + 127, 0) - down, 1)
    scale = np.exp2(byte - 127.0)
    codes = (blocks / scale).astype(np.float32).astype(dtype).astype(np.float64)
    return np.moveaxis((codes * scale).reshape(v.shape), -1, axis)


WIDE = False


def mx_kscale(k):
    if not WIDE:
        return np.ones(k)
    levels = np.array([10, -10, 5, -5, 0])
    if k % 512:
        return np.exp2(np.random.permutation(np.resize(levels, k // 32))).repeat(32)
    a = np.empty((k // 512, 16))
    for p in range(k // 512):
        a[p, :8] = np.random.permutation(np.resize(levels, 8))
        for g in range(8):
            far = levels[np.abs(levels - a[p, g]) >= 10]
            a[p, g + 8] = far[np.random.randint(len(far))]
    return np.exp2(a.ravel()).repeat(32)


def f64(x):
    return np.asarray(x).astype(np.float64)


def striped(idx):
    return np.tile(idx.reshape(-1, 16).T, (8, 1)).astype(np.uint16)


def unstriped(offs):
    return offs[:16].T.reshape(-1).astype(np.int64)


E2M1 = np.array([0.0, 0.5, 1.0, 1.5, 2.0, 3.0, 4.0, 6.0, -0.0, -0.5, -1.0, -1.5, -2.0, -3.0, -4.0, -6.0])


def pack_fp4(w):
    k, n = w.shape
    w = f64(np.asarray(w, np.float32).astype(ml_dtypes.bfloat16)).reshape(k // 32, 32, n)
    amax = np.abs(w).max(1)
    mant, ex = np.frexp(amax / 6.0)
    byte = np.clip(np.where(amax > 0, np.where(mant > 0.5, ex, ex - 1) + 127, 1), 1, 254)
    scaled = (w * np.exp2(127.0 - byte)[:, None, :]).reshape(k, n).astype(np.float32)
    c = np.ascontiguousarray(scaled.reshape(k // 512, 128, 4, n).transpose(0, 1, 3, 2)).astype(ml_dtypes.float4_e2m1fn).view(np.uint8) & 0xF
    words = (c[..., 0::2] | (c[..., 1::2] << 4)).reshape(k // 512, 128, 2 * n)
    return np.ascontiguousarray(words), np.ascontiguousarray(byte.astype(np.uint8).reshape(k // 512, 16, n))


def unpack_fp4(words, scales):
    g, _, n = scales.shape
    words = np.ascontiguousarray(words).reshape(g, 128, n, 2)
    nib = np.empty((g, 128, n, 4), np.uint8)
    nib[..., 0::2] = words & 0xF
    nib[..., 1::2] = words >> 4
    vals = E2M1[nib] * np.repeat(np.exp2(scales.astype(np.float64) - 127.0), 8, axis=1)[..., None]
    return vals.transpose(0, 1, 3, 2).reshape(g * 512, n)


def gelu(v):
    return 0.5 * v * (1.0 + np.tanh(np.sqrt(2.0 / np.pi) * (v + 0.044715 * v**3)))


K, T, S, H, N = 1024, 1024, 512, 512, 256
P = 2 ** 7


def setup_inputs():
    n = np.random.standard_normal
    s = mx_kscale(K)[:, None]
    u = mx_kscale(H)
    packed_w2 = pack_fp4(n((H, N)) / np.sqrt(H) / u[:, None])
    return {
        "xT": (n((K, T)) * s).astype(np.float32),
        "w1": (n((K, H)) / np.sqrt(K) / s * u).astype(np.float32),
        "w2_words": packed_w2[0],
        "w2_scales": packed_w2[1],
        "lam": np.tile(np.random.uniform(0.1, 0.9, S), (P, 1)).astype(np.float32),
        "mu": np.tile(np.random.uniform(0.1, 0.9, S), (P, 1)).astype(np.float32),
        "offs": striped(np.random.permutation(T)[:S]),
        "pos1": striped(np.random.permutation(S)),
    }


def reference(xT, w1, w2_words, w2_scales, lam, mu, offs, pos1):
    xq = mxq(f64(xT)[:, unstriped(offs)], 0, "e4m3")
    h = gelu(mxq(f64(w1), 0, "e4m3").T @ xq)
    z = h * f64(lam)[:1] + h[:, unstriped(pos1)] * f64(mu)[:1]
    return unpack_fp4(w2_words, w2_scales).T @ mxq(z, 0, "e4m3")

@@ -1,0 +1,220 @@
+from contextlib import ExitStack
+
+import concourse.mybir as mybir
+from concourse.masks import make_identity
+
+K, T, S, H, N = 1024, 1024, 512, 512, 256
+FLOPS = 2 * K * H * S + 2 * H * N * S
+
+F32 = mybir.dt.float32
+BF16 = mybir.dt.bfloat16
+I32 = mybir.dt.int32
+U32 = mybir.dt.uint32
+U16 = mybir.dt.uint16
+U8 = mybir.dt.uint8
+FP8X4 = mybir.dt.float8_e4m3fn_x4
+FP4X4 = mybir.dt.float4_e2m1fn_x4
+COPY = mybir.ActivationFunctionType.Copy
+GELU = mybir.ActivationFunctionType.Gelu_apprx_tanh
+MULT = mybir.AluOpType.mult
+ADD = mybir.AluOpType.add
+
+P = 128
+PACK = 4
+K_PASS = P * PACK
+PASSES = K // K_PASS
+X_CHUNKS = [[(0, 512, 176), (512, 768, 96), (768, 1024, 96)], [(0, 512, 352), (512, 768, 160), (768, 1024, 112)]]
+W_CHUNK = 256
+BLOCKS = S // P
+SPARE = 8
+LINE = 4
+
+
+def tile_picked_mixup_gelu_e_kernel(
+    tc, xT, w1, w2_words, w2_scales, lam, mu, offs, pos1, out
+):
+    nc = tc.nc
+    with ExitStack() as ctx:
+        keep = ctx.enter_context(tc.tile_pool(name="keep", bufs=1))
+        psum = ctx.enter_context(tc.psum_pool(name="psum", bufs=1))
+
+        def sb(name, shape, dtype, tag=None):
+            return keep.tile(shape, dtype, name=name, tag=tag or name, align_bytes=64)
+
+        def bank(index):
+            return psum.tile([P, S], F32, name="bank%d" % index)
+
+        offs_sb = keep.tile([P, S // 16], U16, name="offs_sb")
+        pos_sb = keep.tile([P, S // 16], U16, name="pos_sb")
+
+        ident = sb("ident", [P, P], F32)
+        lam_rows = sb("lam_rows", [P, P], F32)
+        x_bytes = sb("x_bytes", [P, T], U8)
+        w2_bytes = sb("w2_bytes", [P, N], U8)
+        h = [sb("h%d" % t, [P, S + SPARE], F32) for t in range(PACK)]
+        warm = sb("warm", [P, 8], F32)
+        nc.gpsimd.memset(lam_rows[:], 0.0)
+        nc.gpsimd.memset(x_bytes[:].bitcast(I32), 0)
+        nc.gpsimd.memset(w2_bytes[:], 0)
+        for t in range(PACK):
+            nc.gpsimd.memset(h[t][:, S:], 0.0)
+        make_identity(nc, ident[:])
+        nc.scalar.activation(out=warm[:], in_=h[0][:, S:], func=GELU)
+
+        x_rows = xT.rearrange("(g p j) c -> g p j c", p=P, j=PACK)
+        w_rows = w1.rearrange("(g p j) c -> g p j c", p=P, j=PACK)
+        x_raw = {}
+        w_raw = {}
+        for g in range(PASSES):
+            for c0, c1, cut in X_CHUNKS[g]:
+                x_raw[g, c0] = sb("x_raw%d_%d" % (g, c0), [P, PACK, c1 - c0], F32)
+                nc.sync.dma_start(out=x_raw[g, c0][:], in_=x_rows[g, :, :, c0:c1])
+            if g == 0:
+                nc.sync.dma_start(offs_sb[:], offs)
+                nc.sync.dma_start(out=lam_rows[0:BLOCKS, :], in_=lam[0:1, :].rearrange("o (b j) -> (o b) j", j=P))
+        for g in range(PASSES):
+            for c in range(H // W_CHUNK):
+                w_raw[g, c] = sb("w_raw%d%d" % (g, c), [P, PACK, W_CHUNK], F32)
+                nc.sync.dma_start(out=w_raw[g, c][:], in_=w_rows[g, :, :, c * W_CHUNK : (c + 1) * W_CHUNK])
+        nc.sync.dma_start(pos_sb[:], pos1)
+        mu_sb = sb("mu_sb", [P, S], F32)
+        nc.sync.dma_start(out=mu_sb[:], in_=mu)
+        w2_codes = sb("w2_codes", [P, 2 * N], U8)
+        nc.sync.dma_start(out=w2_codes[:].bitcast(I32), in_=w2_words[0].bitcast(I32))
+        for q in range(4):
+            nc.sync.dma_start(
+                out=w2_bytes[32 * q : 32 * q + 4, :].bitcast(I32),
+                in_=w2_scales[0, 4 * q : 4 * q + 4, :].bitcast(I32),
+            )
+
+        lam_bank = bank(7)
+        nc.tensor.transpose(lam_bank[:, 0:P], lam_rows[:], ident[:])
+        lam_cols = sb("lam_cols", [P, BLOCKS], F32)
+        nc.scalar.activation(out=lam_cols[:], in_=lam_bank[:, 0:BLOCKS], func=COPY)
+
+        x_words = [sb("x_words%d" % g, [P, T], U32) for g in range(PASSES)]
+        picked_words = [sb("picked_words0", [P, S], U32)]
+        picked_bytes = sb("picked_bytes", [P, S], U8)
+        for g in range(PASSES):
+            for c0, c1, cut in X_CHUNKS[g]:
+                grouped = sb("x_grouped%d_%d" % (g, c0), [P, c1 - c0, PACK], BF16)
+                src = x_raw[g, c0][:].rearrange("p j (c i) -> p c j i", i=LINE)
+                dst = grouped[:].rearrange("p (c i) j -> p c j i", i=LINE)
+                nc.scalar.activation(out=dst[:, : cut // LINE], in_=src[:, : cut // LINE], func=COPY)
+                nc.vector.tensor_copy(out=dst[:, cut // LINE :], in_=src[:, cut // LINE :])
+                nc.vector.quantize_mx(
+                    out=x_words[g][:, c0:c1].bitcast(FP8X4),
+                    scales=x_bytes[4 * g :, c0:c1],
+                    in_=grouped[:].rearrange("p c j -> p (c j)"),
+                )
+            if g == 0:
+                nc.vector.tensor_copy(out=picked_words[g][:], in_=x_words[g][:].indirect(offs_sb[:]))
+        nc.vector.tensor_copy(out=picked_bytes[:], in_=x_bytes[:].indirect(offs_sb[:]))
+
+        half = PACK // 2
+        m_chunk = W_CHUNK // PACK
+        early = [sb("w_early%d" % g, [P, half, P, PACK], BF16) for g in range(PASSES)]
+        late = sb("w_late", [P, half, PASSES, P, PACK], BF16)
+        w_words = {}
+        w_bytes = {}
+
+        def quantise_w(name, values, keys):
+            words = sb("w_words" + name, [P, len(keys) * P], U32)
+            planes = sb("w_bytes" + name, [P, len(keys) * P], U8)
+            nc.vector.quantize_mx(out=words[:].bitcast(FP8X4), scales=planes[:], in_=values)
+            for n, key in enumerate(keys):
+                w_words[key] = words[:, n * P : (n + 1) * P]
+                w_bytes[key] = planes[:, n * P : (n + 1) * P]
+
+        for g in range(PASSES):
+            for c in range(H // W_CHUNK):
+                src = w_raw[g, c][:].rearrange("p j (m t) -> p m j t", t=PACK)
+                ms = slice(c * m_chunk, (c + 1) * m_chunk)
+                dst = early[g][:, :, ms, :].rearrange("p t m j -> p m j t")
+                if g == PASSES - 1 and c == H // W_CHUNK - 1:
+                    nc.vector.tensor_copy(out=dst, in_=src[:, :, :, :half])
+                else:
+                    nc.scalar.activation(out=dst, in_=src[:, :, :, :half], func=COPY)
+                dst = late[:, :, g, ms, :].rearrange("p t m j -> p m j t")
+                nc.scalar.activation(out=dst, in_=src[:, :, :, half:], func=COPY)
+            if g == 0:
+                quantise_w("e0", early[g][:].rearrange("p t m j -> p (t m j)"), [(0, g), (1, g)])
+                picked_words.append(sb("picked_words1", [P, S], U32, tag="w_early0"))
+                nc.vector.tensor_copy(out=picked_words[1][:], in_=x_words[1][:].indirect(offs_sb[:]))
+            else:
+                for t in range(half):
+                    quantise_w("e1%d" % t, early[g][:, t].rearrange("p m j -> p (m j)"), [(t, g)])
+        for t in range(half, PACK):
+            quantise_w("l%d" % t, late[:, t - half].rearrange("p g m j -> p (g m j)"), [(t, 0), (t, 1)])
+
+        partner = sb("partner", [P, PACK, S], F32)
+        for t in range(PACK):
+            pieces = [(0, 0, S // 2), (PACK, S // 2, S)] if t == 0 else [(t, 0, S)]
+            accs = [bank(index) for index, c0, c1 in pieces]
+            for g in range(PASSES):
+                for acc, (index, c0, c1) in zip(accs, pieces):
+                    nc.tensor.matmul_mx(
+                        out=acc[:, : c1 - c0],
+                        lhsT=w_words[t, g].bitcast(FP8X4),
+                        lhsT_scale=w_bytes[t, g],
+                        rhs=picked_words[g][:, c0:c1].bitcast(FP8X4),
+                        rhs_scale=picked_bytes[4 * g :, c0:c1],
+                        start=(g == 0),
+                        stop=(g == PASSES - 1),
+                    )
+            for acc, (index, c0, c1) in zip(accs, pieces):
+                nc.scalar.activation(out=h[t][:, c0:c1], in_=acc[:, : c1 - c0], func=GELU)
+            nc.vector.tensor_tensor(out=partner[:, t, :], in0=h[t][:].indirect(pos_sb[:]), in1=mu_sb[:], op=MULT)
+
+        turned = []
+        for b in range(BLOCKS):
+            turned.append(bank(PACK + b))
+            for t in range(PACK):
+                nc.tensor.transpose(turned[b][:, t * P : (t + 1) * P], h[t][:, b * P : (b + 1) * P], ident[:])
+        own = []
+        for b in range(BLOCKS):
+            scaled = sb("scaled%d" % b, [P, S], F32)
+            nc.scalar.activation(out=scaled[:], in_=turned[b][:], func=COPY, scale=lam_cols[:, b : b + 1])
+            own.append(bank(b))
+            for t in range(PACK):
+                nc.tensor.transpose(own[b][:, t * P : (t + 1) * P], scaled[:, t * P : (t + 1) * P], ident[:])
+
+        out_rows = out.rearrange("(a m) j -> m a j", m=P)
+        z = [sb("z%d" % b, [P, P, PACK], BF16) for b in range(BLOCKS)]
+
+        def mix(b):
+            nc.vector.tensor_tensor(
+                out=z[b][:].rearrange("p (c i) t -> p c t i", i=LINE),
+                in0=own[b][:].rearrange("p (t c i) -> p c t i", t=PACK, i=LINE),
+                in1=partner[:, :, b * P : (b + 1) * P].rearrange("p t (c i) -> p c t i", i=LINE),
+                op=ADD,
+            )
+
+        def finish(b):
+            z_words = sb("z_words%d" % b, [P, P], U32)
+            z_bytes = sb("z_bytes%d" % b, [P, P], U8)
+            nc.vector.quantize_mx(
+                out=z_words[:].bitcast(FP8X4), scales=z_bytes[:], in_=z[b][:].rearrange("p j t -> p (j t)")
+            )
+            res = bank(PACK + b)
+            for a in range(N // P):
+                nc.tensor.matmul_mx(
+                    out=res[:, a * P : (a + 1) * P],
+                    lhsT=w2_codes[:, 2 * a * P : 2 * (a + 1) * P].bitcast(FP4X4),
+                    lhsT_scale=w2_bytes[:, a * P : (a + 1) * P],
+                    rhs=z_words[:].bitcast(FP8X4),
+                    rhs_scale=z_bytes[:],
+                    start=True,
+                    stop=True,
+                )
+            staged = sb("staged%d" % b, [P, N], F32)
+            nc.scalar.activation(out=staged[:], in_=res[:, :N], func=COPY)
+            nc.sync.dma_start(
+                out=out_rows[:, :, b * P : (b + 1) * P], in_=staged[:].rearrange("p (a j) -> p a j", j=P)
+            )
+
+        mix(0)
+        for b in range(1, BLOCKS):
+            mix(b)
+            finish(b - 1)
+        finish(BLOCKS - 1)

@@ -23,8 +23,8 @@ P = 128
 PACK = 4
 K_PASS = P * PACK
 PASSES = K // K_PASS
-X_CHUNKS = [[(0, 512, 176), (512, 768, 96), (768, 1024, 96)], [(0, 512, 352), (512, 768, 160), (768, 1024, 112)]]
-W_CHUNK = 256
+PAIR = 2
+X_ON_SCALAR = [344, 344, 1024, 640]
 BLOCKS = S // P
 SPARE = 8
 LINE = 4
@@ -49,12 +49,10 @@ def tile_picked_mixup_gelu_e_kernel(
 
         ident = sb("ident", [P, P], F32)
         lam_rows = sb("lam_rows", [P, P], F32)
-        x_bytes = sb("x_bytes", [P, T], U8)
         w2_bytes = sb("w2_bytes", [P, N], U8)
         h = [sb("h%d" % t, [P, S + SPARE], F32) for t in range(PACK)]
         warm = sb("warm", [P, 8], F32)
         nc.gpsimd.memset(lam_rows[:], 0.0)
-        nc.gpsimd.memset(x_bytes[:].bitcast(I32), 0)
         nc.gpsimd.memset(w2_bytes[:], 0)
         for t in range(PACK):
             nc.gpsimd.memset(h[t][:, S:], 0.0)
@@ -66,16 +64,16 @@ def tile_picked_mixup_gelu_e_kernel(
         x_raw = {}
         w_raw = {}
         for g in range(PASSES):
-            for c0, c1, cut in X_CHUNKS[g]:
-                x_raw[g, c0] = sb("x_raw%d_%d" % (g, c0), [P, PACK, c1 - c0], F32)
-                nc.sync.dma_start(out=x_raw[g, c0][:], in_=x_rows[g, :, :, c0:c1])
+            for u in range(PACK // PAIR):
+                x_raw[g, u] = sb("x_raw%d%d" % (g, u), [P, PAIR, T], F32)
+                nc.sync.dma_start(out=x_raw[g, u][:], in_=x_rows[g, :, PAIR * u : PAIR * (u + 1), :])
+                if g == 0 and u == 0:
+                    nc.sync.dma_start(offs_sb[:], offs)
             if g == 0:
-                nc.sync.dma_start(offs_sb[:], offs)
-                nc.sync.dma_start(out=lam_rows[0:BLOCKS, :], in_=lam[0:1, :].rearrange("o (b j) -> (o b) j", j=P))
+                nc.scalar.dma_start(out=lam_rows[0:BLOCKS, :], in_=lam[0:1, :].rearrange("o (b j) -> (o b) j", j=P))
         for g in range(PASSES):
-            for c in range(H // W_CHUNK):
-                w_raw[g, c] = sb("w_raw%d%d" % (g, c), [P, PACK, W_CHUNK], F32)
-                nc.sync.dma_start(out=w_raw[g, c][:], in_=w_rows[g, :, :, c * W_CHUNK : (c + 1) * W_CHUNK])
+            w_raw[g] = sb("w_raw%d" % g, [P, PACK, H], F32)
+            nc.sync.dma_start(out=w_raw[g][:], in_=w_rows[g])
         nc.sync.dma_start(pos_sb[:], pos1)
         mu_sb = sb("mu_sb", [P, S], F32)
         nc.sync.dma_start(out=mu_sb[:], in_=mu)
@@ -92,60 +90,68 @@ def tile_picked_mixup_gelu_e_kernel(
         lam_cols = sb("lam_cols", [P, BLOCKS], F32)
         nc.scalar.activation(out=lam_cols[:], in_=lam_bank[:, 0:BLOCKS], func=COPY)
 
-        x_words = [sb("x_words%d" % g, [P, T], U32) for g in range(PASSES)]
-        picked_words = [sb("picked_words0", [P, S], U32)]
-        picked_bytes = sb("picked_bytes", [P, S], U8)
-        for g in range(PASSES):
-            for c0, c1, cut in X_CHUNKS[g]:
-                grouped = sb("x_grouped%d_%d" % (g, c0), [P, c1 - c0, PACK], BF16)
-                src = x_raw[g, c0][:].rearrange("p j (c i) -> p c j i", i=LINE)
-                dst = grouped[:].rearrange("p (c i) j -> p c j i", i=LINE)
-                nc.scalar.activation(out=dst[:, : cut // LINE], in_=src[:, : cut // LINE], func=COPY)
-                nc.vector.tensor_copy(out=dst[:, cut // LINE :], in_=src[:, cut // LINE :])
-                nc.vector.quantize_mx(
-                    out=x_words[g][:, c0:c1].bitcast(FP8X4),
-                    scales=x_bytes[4 * g :, c0:c1],
-                    in_=grouped[:].rearrange("p c j -> p (c j)"),
-                )
-            if g == 0:
-                nc.vector.tensor_copy(out=picked_words[g][:], in_=x_words[g][:].indirect(offs_sb[:]))
-        nc.vector.tensor_copy(out=picked_bytes[:], in_=x_bytes[:].indirect(offs_sb[:]))
-
-        half = PACK // 2
-        m_chunk = W_CHUNK // PACK
-        early = [sb("w_early%d" % g, [P, half, P, PACK], BF16) for g in range(PASSES)]
-        late = sb("w_late", [P, half, PASSES, P, PACK], BF16)
+        x_words = {}
+        x_bytes = {}
         w_words = {}
         w_bytes = {}
+        half = PACK // 2
 
-        def quantise_w(name, values, keys):
+        def pick(g):
+            picked = sb("picked%d" % g, [P, PACK // PAIR, S], U32)
+            for u in range(PACK // PAIR):
+                n = PASSES * g + u
+                pairs = sb("x_pairs%d" % n, [P, T * PAIR], BF16, tag=["x_pairs", "x_pairs", "x_raw01", "x_grouped0"][n])
+                cut = X_ON_SCALAR[PASSES * g + u] // LINE
+                src = x_raw[g, u][:].rearrange("p e (c i) -> p c e i", i=LINE)
+                dst = pairs[:].rearrange("p (c i e) -> p c e i", i=LINE, e=PAIR)
+                if cut:
+                    nc.scalar.activation(out=dst[:, :cut], in_=src[:, :cut], func=COPY)
+                if cut < T // LINE:
+                    nc.vector.tensor_copy(out=dst[:, cut:], in_=src[:, cut:])
+                nc.vector.tensor_copy(out=picked[:, u, :], in_=pairs[:].bitcast(U32).indirect(offs_sb[:]))
+            grouped = sb("x_grouped%d" % g, [P, S * PACK], BF16)
+            nc.vector.tensor_copy(
+                out=grouped[:].bitcast(I32).rearrange("p (c i u) -> p c u i", i=PAIR, u=PACK // PAIR),
+                in_=picked[:].bitcast(I32).rearrange("p u (c i) -> p c u i", i=PAIR),
+            )
+            return grouped
+
+        def quantise(words, planes, values):
+            nc.vector.quantize_mx(out=words.bitcast(FP8X4), scales=planes, in_=values)
+
+        def quantise_x(g, grouped, tag=None):
+            x_words[g] = sb("x_words%d" % g, [P, S], U32, tag=tag)
+            x_bytes[g] = sb("x_bytes%d" % g, [P, S], U8)
+            quantise(x_words[g][:], x_bytes[g][:], grouped[:])
+
+        def w_tiles(name, keys):
             words = sb("w_words" + name, [P, len(keys) * P], U32)
             planes = sb("w_bytes" + name, [P, len(keys) * P], U8)
-            nc.vector.quantize_mx(out=words[:].bitcast(FP8X4), scales=planes[:], in_=values)
             for n, key in enumerate(keys):
                 w_words[key] = words[:, n * P : (n + 1) * P]
                 w_bytes[key] = planes[:, n * P : (n + 1) * P]
+            return words[:], planes[:]
 
-        for g in range(PASSES):
-            for c in range(H // W_CHUNK):
-                src = w_raw[g, c][:].rearrange("p j (m t) -> p m j t", t=PACK)
-                ms = slice(c * m_chunk, (c + 1) * m_chunk)
-                dst = early[g][:, :, ms, :].rearrange("p t m j -> p m j t")
-                if g == PASSES - 1 and c == H // W_CHUNK - 1:
-                    nc.vector.tensor_copy(out=dst, in_=src[:, :, :, :half])
-                else:
-                    nc.scalar.activation(out=dst, in_=src[:, :, :, :half], func=COPY)
-                dst = late[:, :, g, ms, :].rearrange("p t m j -> p m j t")
-                nc.scalar.activation(out=dst, in_=src[:, :, :, half:], func=COPY)
-            if g == 0:
-                quantise_w("e0", early[g][:].rearrange("p t m j -> p (t m j)"), [(0, g), (1, g)])
-                picked_words.append(sb("picked_words1", [P, S], U32, tag="w_early0"))
-                nc.vector.tensor_copy(out=picked_words[1][:], in_=x_words[1][:].indirect(offs_sb[:]))
-            else:
-                for t in range(half):
-                    quantise_w("e1%d" % t, early[g][:, t].rearrange("p m j -> p (m j)"), [(t, g)])
+        w_src = [w_raw[g][:].rearrange("p j (m t) -> p m j t", t=PACK) for g in range(PASSES)]
+
+        quantise_x(0, pick(0))
+        grouped = pick(1)
+
+        dealt = sb("w_dealt", [P, (1 + PASSES) * half * K_PASS], BF16, tag="x_raw11")
+        early = dealt[:, : half * K_PASS].rearrange("p (t m j) -> p t m j", t=half, j=PACK)
+        late = dealt[:, half * K_PASS :].rearrange("p (t g m j) -> p t g m j", t=half, g=PASSES, j=PACK)
+        nc.scalar.activation(out=early.rearrange("p t m j -> p m j t"), in_=w_src[0][:, :, :, :half], func=COPY)
+        nc.scalar.activation(out=late[:, :, 0].rearrange("p t m j -> p m j t"), in_=w_src[0][:, :, :, half:], func=COPY)
+        quantise(*w_tiles("e0", [(0, 0), (1, 0)]), dealt[:, : half * K_PASS])
+        quantise_x(1, grouped)
+
+        early = sb("w_early1", [P, half, P, PACK], BF16, tag="w_raw0")
+        nc.scalar.activation(out=early[:].rearrange("p t m j -> p m j t"), in_=w_src[1][:, :, :, :half], func=COPY)
+        nc.scalar.activation(out=late[:, :, 1].rearrange("p t m j -> p m j t"), in_=w_src[1][:, :, :, half:], func=COPY)
+        for t in range(half):
+            quantise(*w_tiles("e1%d" % t, [(t, 1)]), early[:, t].rearrange("p m j -> p (m j)"))
         for t in range(half, PACK):
-            quantise_w("l%d" % t, late[:, t - half].rearrange("p g m j -> p (g m j)"), [(t, 0), (t, 1)])
+            quantise(*w_tiles("l%d" % t, [(t, 0), (t, 1)]), late[:, t - half].rearrange("p g m j -> p (g m j)"))
 
         partner = sb("partner", [P, PACK, S], F32)
         for t in range(PACK):
@@ -157,8 +163,8 @@ def tile_picked_mixup_gelu_e_kernel(
                         out=acc[:, : c1 - c0],
                         lhsT=w_words[t, g].bitcast(FP8X4),
                         lhsT_scale=w_bytes[t, g],
-                        rhs=picked_words[g][:, c0:c1].bitcast(FP8X4),
-                        rhs_scale=picked_bytes[4 * g :, c0:c1],
+                        rhs=x_words[g][:, c0:c1].bitcast(FP8X4),
+                        rhs_scale=x_bytes[g][:, c0:c1],
                         start=(g == 0),
                         stop=(g == PASSES - 1),
                     )
@@ -184,9 +190,9 @@ def tile_picked_mixup_gelu_e_kernel(
 
         def mix(b):
             nc.vector.tensor_tensor(
-                out=z[b][:].rearrange("p (c i) t -> p c t i", i=LINE),
-                in0=own[b][:].rearrange("p (t c i) -> p c t i", t=PACK, i=LINE),
-                in1=partner[:, :, b * P : (b + 1) * P].rearrange("p t (c i) -> p c t i", i=LINE),
+                out=z[b][:].rearrange("p (c i) t -> p c t i", i=PAIR),
+                in0=own[b][:].rearrange("p (t c i) -> p c t i", t=PACK, i=PAIR),
+                in1=partner[:, :, b * P : (b + 1) * P].rearrange("p t (c i) -> p c t i", i=PAIR),
                 op=ADD,
             )
 

@@ -109,12 +109,13 @@ def tile_picked_mixup_gelu_e_kernel(
                 if cut < T // LINE:
                     nc.vector.tensor_copy(out=dst[:, cut:], in_=src[:, cut:])
                 nc.vector.tensor_copy(out=picked[:, u, :], in_=pairs[:].bitcast(U32).indirect(offs_sb[:]))
-            grouped = sb("x_grouped%d" % g, [P, S * PACK], BF16)
+            return picked
+
+        def weave(grouped, picked):
             nc.vector.tensor_copy(
-                out=grouped[:].bitcast(I32).rearrange("p (c i u) -> p c u i", i=PAIR, u=PACK // PAIR),
-                in_=picked[:].bitcast(I32).rearrange("p u (c i) -> p c u i", i=PAIR),
+                out=grouped.bitcast(I32).rearrange("p (c i u) -> p c u i", i=PAIR, u=PACK // PAIR),
+                in_=picked.bitcast(I32).rearrange("p u (c i) -> p c u i", i=PAIR),
             )
-            return grouped
 
         def quantise(words, planes, values):
             nc.vector.quantize_mx(out=words.bitcast(FP8X4), scales=planes, in_=values)
@@ -122,7 +123,7 @@ def tile_picked_mixup_gelu_e_kernel(
         def quantise_x(g, grouped, tag=None):
             x_words[g] = sb("x_words%d" % g, [P, S], U32, tag=tag)
             x_bytes[g] = sb("x_bytes%d" % g, [P, S], U8)
-            quantise(x_words[g][:], x_bytes[g][:], grouped[:])
+            quantise(x_words[g][:], x_bytes[g][:], grouped)
 
         def w_tiles(name, keys):
             words = sb("w_words" + name, [P, len(keys) * P], U32)
@@ -134,16 +135,24 @@ def tile_picked_mixup_gelu_e_kernel(
 
         w_src = [w_raw[g][:].rearrange("p j (m t) -> p m j t", t=PACK) for g in range(PASSES)]
 
-        quantise_x(0, pick(0))
-        grouped = pick(1)
+        grouped = sb("x_grouped0", [P, S * PACK], BF16)
+        weave(grouped[:], pick(0)[:])
+        quantise_x(0, grouped[:])
+        picked = pick(1)
 
-        dealt = sb("w_dealt", [P, (1 + PASSES) * half * K_PASS], BF16, tag="x_raw11")
+        dealt = sb("w_dealt", [P, S * PACK + PASSES * half * K_PASS], BF16, tag="x_raw11")
         early = dealt[:, : half * K_PASS].rearrange("p (t m j) -> p t m j", t=half, j=PACK)
-        late = dealt[:, half * K_PASS :].rearrange("p (t g m j) -> p t g m j", t=half, g=PASSES, j=PACK)
+        late = dealt[:, S * PACK :].rearrange("p (t g m j) -> p t g m j", t=half, g=PASSES, j=PACK)
         nc.scalar.activation(out=early.rearrange("p t m j -> p m j t"), in_=w_src[0][:, :, :, :half], func=COPY)
         nc.scalar.activation(out=late[:, :, 0].rearrange("p t m j -> p m j t"), in_=w_src[0][:, :, :, half:], func=COPY)
         quantise(*w_tiles("e0", [(0, 0), (1, 0)]), dealt[:, : half * K_PASS])
-        quantise_x(1, grouped)
+        x_words[1] = sb("x_words1", [P, S], U32)
+        x_bytes[1] = sb("x_bytes1", [P, S], U8)
+        halves = [slice(S // 2, S), slice(0, S // 2)]
+        for cols in halves:
+            weave(dealt[:, PACK * cols.start : PACK * cols.stop], picked[:, :, cols])
+        for cols in halves:
+            quantise(x_words[1][:, cols], x_bytes[1][:, cols], dealt[:, PACK * cols.start : PACK * cols.stop])
 
         early = sb("w_early1", [P, half, P, PACK], BF16, tag="w_raw0")
         nc.scalar.activation(out=early[:].rearrange("p t m j -> p m j t"), in_=w_src[1][:, :, :, :half], func=COPY)
@@ -155,7 +164,7 @@ def tile_picked_mixup_gelu_e_kernel(
 
         partner = sb("partner", [P, PACK, S], F32)
         for t in range(PACK):
-            pieces = [(0, 0, S // 2), (PACK, S // 2, S)] if t == 0 else [(t, 0, S)]
+            pieces = [(PACK, S // 2, S), (0, 0, S // 2)] if t == 0 else [(t, 0, S)]
             accs = [bank(index) for index, c0, c1 in pieces]
             for g in range(PASSES):
                 for acc, (index, c0, c1) in zip(accs, pieces):

@@ -133,6 +133,9 @@ def tile_picked_mixup_gelu_e_kernel(
                 w_bytes[key] = planes[:, n * P : (n + 1) * P]
             return words[:], planes[:]
 
+        def by_tile(values):
+            return values.rearrange("p (t m j) -> p m j t", t=half, j=PACK)
+
         w_src = [w_raw[g][:].rearrange("p j (m t) -> p m j t", t=PACK) for g in range(PASSES)]
 
         grouped = sb("x_grouped0", [P, S * PACK], BF16)
@@ -140,12 +143,12 @@ def tile_picked_mixup_gelu_e_kernel(
         quantise_x(0, grouped[:])
         picked = pick(1)
 
-        dealt = sb("w_dealt", [P, S * PACK + PASSES * half * K_PASS], BF16, tag="x_raw11")
-        early = dealt[:, : half * K_PASS].rearrange("p (t m j) -> p t m j", t=half, j=PACK)
-        late = dealt[:, S * PACK :].rearrange("p (t g m j) -> p t g m j", t=half, g=PASSES, j=PACK)
-        nc.scalar.activation(out=early.rearrange("p t m j -> p m j t"), in_=w_src[0][:, :, :, :half], func=COPY)
-        nc.scalar.activation(out=late[:, :, 0].rearrange("p t m j -> p m j t"), in_=w_src[0][:, :, :, half:], func=COPY)
-        quantise(*w_tiles("e0", [(0, 0), (1, 0)]), dealt[:, : half * K_PASS])
+        dealt = sb("w_dealt0", [P, S * PACK + half * K_PASS], BF16, tag="x_raw11")
+        early = dealt[:, : half * K_PASS]
+        late = dealt[:, S * PACK :]
+        nc.scalar.activation(out=by_tile(early), in_=w_src[0][:, :, :, :half], func=COPY)
+        nc.scalar.activation(out=by_tile(late), in_=w_src[0][:, :, :, half:], func=COPY)
+        quantise(*w_tiles("e0", [(0, 0), (1, 0)]), early)
         x_words[1] = sb("x_words1", [P, S], U32)
         x_bytes[1] = sb("x_bytes1", [P, S], U8)
         halves = [slice(S // 2, S), slice(0, S // 2)]
@@ -153,14 +156,16 @@ def tile_picked_mixup_gelu_e_kernel(
             weave(dealt[:, PACK * cols.start : PACK * cols.stop], picked[:, :, cols])
         for cols in halves:
             quantise(x_words[1][:, cols], x_bytes[1][:, cols], dealt[:, PACK * cols.start : PACK * cols.stop])
+        quantise(*w_tiles("l0", [(2, 0), (3, 0)]), late)
 
-        early = sb("w_early1", [P, half, P, PACK], BF16, tag="w_raw0")
-        nc.scalar.activation(out=early[:].rearrange("p t m j -> p m j t"), in_=w_src[1][:, :, :, :half], func=COPY)
-        nc.scalar.activation(out=late[:, :, 1].rearrange("p t m j -> p m j t"), in_=w_src[1][:, :, :, half:], func=COPY)
+        dealt = sb("w_dealt1", [P, PACK * K_PASS], BF16, tag="w_raw0")
+        early = dealt[:, : half * K_PASS]
+        late = dealt[:, half * K_PASS :]
+        nc.scalar.activation(out=by_tile(early), in_=w_src[1][:, :, :, :half], func=COPY)
+        nc.scalar.activation(out=by_tile(late), in_=w_src[1][:, :, :, half:], func=COPY)
         for t in range(half):
-            quantise(*w_tiles("e1%d" % t, [(t, 1)]), early[:, t].rearrange("p m j -> p (m j)"))
-        for t in range(half, PACK):
-            quantise(*w_tiles("l%d" % t, [(t, 0), (t, 1)]), late[:, t - half].rearrange("p g m j -> p (g m j)"))
+            quantise(*w_tiles("e1%d" % t, [(t, 1)]), early[:, t * K_PASS : (t + 1) * K_PASS])
+        quantise(*w_tiles("l1", [(2, 1), (3, 1)]), late)
 
         partner = sb("partner", [P, PACK, S], F32)
         for t in range(PACK):

@@ -149,13 +149,8 @@ def tile_picked_mixup_gelu_e_kernel(
         nc.scalar.activation(out=by_tile(early), in_=w_src[0][:, :, :, :half], func=COPY)
         nc.scalar.activation(out=by_tile(late), in_=w_src[0][:, :, :, half:], func=COPY)
         quantise(*w_tiles("e0", [(0, 0), (1, 0)]), early)
-        x_words[1] = sb("x_words1", [P, S], U32)
-        x_bytes[1] = sb("x_bytes1", [P, S], U8)
-        halves = [slice(S // 2, S), slice(0, S // 2)]
-        for cols in halves:
-            weave(dealt[:, PACK * cols.start : PACK * cols.stop], picked[:, :, cols])
-        for cols in halves:
-            quantise(x_words[1][:, cols], x_bytes[1][:, cols], dealt[:, PACK * cols.start : PACK * cols.stop])
+        weave(dealt[:, : S * PACK], picked[:])
+        quantise_x(1, dealt[:, : S * PACK])
         quantise(*w_tiles("l0", [(2, 0), (3, 0)]), late)
 
         dealt = sb("w_dealt1", [P, PACK * K_PASS], BF16, tag="w_raw0")
@@ -169,7 +164,7 @@ def tile_picked_mixup_gelu_e_kernel(
 
         partner = sb("partner", [P, PACK, S], F32)
         for t in range(PACK):
-            pieces = [(PACK, S // 2, S), (0, 0, S // 2)] if t == 0 else [(t, 0, S)]
+            pieces = [(0, 0, S // 2), (PACK, S // 2, S)] if t == 0 else [(t, 0, S)]
             accs = [bank(index) for index, c0, c1 in pieces]
             for g in range(PASSES):
                 for acc, (index, c0, c1) in zip(accs, pieces):

@@ -18,16 +18,22 @@ COPY = mybir.ActivationFunctionType.Copy
 GELU = mybir.ActivationFunctionType.Gelu_apprx_tanh
 MULT = mybir.AluOpType.mult
 ADD = mybir.AluOpType.add
+IS_LE = mybir.AluOpType.is_le
+MAX = mybir.AluOpType.max
 
 P = 128
 PACK = 4
 K_PASS = P * PACK
 PASSES = K // K_PASS
 PAIR = 2
-X_ON_SCALAR = [344, 344, 1024, 640]
+X_ON_VECTOR = [344, 344, 0, 344]
 BLOCKS = S // P
+TILES = H // P
+HALF = H // 2
 SPARE = 8
 LINE = 4
+TINY = 2.0**-60
+HUGE = 2.0**120
 
 
 def tile_picked_mixup_gelu_e_kernel(
@@ -48,35 +54,47 @@ def tile_picked_mixup_gelu_e_kernel(
         pos_sb = keep.tile([P, S // 16], U16, name="pos_sb")
 
         ident = sb("ident", [P, P], F32)
-        lam_rows = sb("lam_rows", [P, P], F32)
+        share_rows = sb("share_rows", [P, P], F32)
         w2_bytes = sb("w2_bytes", [P, N], U8)
-        h = [sb("h%d" % t, [P, S + SPARE], F32) for t in range(PACK)]
+        h = [sb("h%d" % t, [P, S + SPARE], F32) for t in range(TILES)]
         warm = sb("warm", [P, 8], F32)
-        nc.gpsimd.memset(lam_rows[:], 0.0)
-        nc.gpsimd.memset(w2_bytes[:], 0)
-        for t in range(PACK):
-            nc.gpsimd.memset(h[t][:, S:], 0.0)
+        loaded_rows = sb("loaded_rows", [2 * BLOCKS, P], F32)
+        nc.sync.dma_start(out=loaded_rows[0:BLOCKS, :], in_=lam[0:1, :].rearrange("o (b j) -> (o b) j", j=P))
+        nc.sync.dma_start(out=loaded_rows[BLOCKS:, :], in_=mu[0:1, :].rearrange("o (b j) -> (o b) j", j=P))
+        nc.vector.memset(share_rows[:], 0.0)
+        floor = sb("floor", [2 * BLOCKS, P], F32)
+        nc.vector.tensor_scalar(
+            out=floor[:], in0=loaded_rows[:], scalar1=-TINY, scalar2=-HUGE, op0=IS_LE, op1=MULT
+        )
+        nc.vector.scalar_tensor_tensor(
+            out=share_rows[0 : 2 * BLOCKS, :], in0=floor[:], scalar=TINY, in1=loaded_rows[:], op0=ADD, op1=MAX
+        )
+        for t in range(TILES):
+            nc.vector.memset(h[t][:, S:], 0.0)
         make_identity(nc, ident[:])
+        nc.vector.memset(w2_bytes[:].bitcast(I32), 0)
         nc.scalar.activation(out=warm[:], in_=h[0][:, S:], func=GELU)
 
         x_rows = xT.rearrange("(g p j) c -> g p j c", p=P, j=PACK)
         w_rows = w1.rearrange("(g p j) c -> g p j c", p=P, j=PACK)
         x_raw = {}
         w_raw = {}
-        for g in range(PASSES):
-            for u in range(PACK // PAIR):
-                x_raw[g, u] = sb("x_raw%d%d" % (g, u), [P, PAIR, T], F32)
-                nc.sync.dma_start(out=x_raw[g, u][:], in_=x_rows[g, :, PAIR * u : PAIR * (u + 1), :])
-                if g == 0 and u == 0:
-                    nc.sync.dma_start(offs_sb[:], offs)
-            if g == 0:
-                nc.scalar.dma_start(out=lam_rows[0:BLOCKS, :], in_=lam[0:1, :].rearrange("o (b j) -> (o b) j", j=P))
-        for g in range(PASSES):
-            w_raw[g] = sb("w_raw%d" % g, [P, PACK, H], F32)
-            nc.sync.dma_start(out=w_raw[g][:], in_=w_rows[g])
-        nc.sync.dma_start(pos_sb[:], pos1)
-        mu_sb = sb("mu_sb", [P, S], F32)
-        nc.sync.dma_start(out=mu_sb[:], in_=mu)
+        for n in range(2 * PASSES):
+            g, u = divmod(n, 2)
+            for a in (1, 0):
+                x_raw[n, a] = sb("x_raw%d%d" % (n, a), [P, PAIR, T // 2], F32)
+                nc.sync.dma_start(
+                    out=x_raw[n, a][:],
+                    in_=x_rows[g, :, PAIR * u : PAIR * (u + 1), a * (T // 2) : (a + 1) * (T // 2)],
+                )
+            if n == 0:
+                nc.sync.dma_start(offs_sb[:], offs)
+        for a in range(2):
+            for g in range(PASSES):
+                w_raw[a, g] = sb("w_raw%d%d" % (a, g), [P, PACK, HALF], F32)
+                nc.sync.dma_start(out=w_raw[a, g][:], in_=w_rows[g, :, :, a * HALF : (a + 1) * HALF])
+            if a == 0:
+                nc.sync.dma_start(pos_sb[:], pos1)
         w2_codes = sb("w2_codes", [P, 2 * N], U8)
         nc.sync.dma_start(out=w2_codes[:].bitcast(I32), in_=w2_words[0].bitcast(I32))
         for q in range(4):
@@ -85,86 +103,130 @@ def tile_picked_mixup_gelu_e_kernel(
                 in_=w2_scales[0, 4 * q : 4 * q + 4, :].bitcast(I32),
             )
 
-        lam_bank = bank(7)
-        nc.tensor.transpose(lam_bank[:, 0:P], lam_rows[:], ident[:])
+        share_bank = bank(6)
+        nc.tensor.transpose(share_bank[:, 0:P], share_rows[:], ident[:])
+        lam_given = share_bank[:, 0:BLOCKS]
+        mu_given = share_bank[:, BLOCKS : 2 * BLOCKS]
         lam_cols = sb("lam_cols", [P, BLOCKS], F32)
-        nc.scalar.activation(out=lam_cols[:], in_=lam_bank[:, 0:BLOCKS], func=COPY)
+        windows = {}
+
+        def open_windows(g, tag=None):
+            both = sb("x_pairs%d" % g, [P, (2 * T - SPARE) * PAIR], BF16, tag=tag)
+            for u in range(2):
+                windows[2 * g + u] = both[:, u * (T - SPARE) * PAIR : (u * (T - SPARE) + T) * PAIR]
+
+        open_windows(0)
+        inverse = windows[0].bitcast(F32)[:, :BLOCKS]
+        ratio_cols = sb("ratio_cols", [P, BLOCKS], F32)
+        nc.vector.reciprocal(out=inverse, in_=lam_given)
+        nc.vector.tensor_tensor(out=ratio_cols[:], in0=mu_given, in1=inverse, op=MULT)
+        nc.vector.tensor_copy(out=lam_cols[:], in_=lam_given)
+        ratio_bank = bank(7)
+        for b in range(BLOCKS):
+            nc.tensor.transpose(
+                ratio_bank[:, b * P : (b + 1) * P], ratio_cols[:, b : b + 1].to_broadcast([P, P]), ident[:]
+            )
 
         x_words = {}
         x_bytes = {}
         w_words = {}
         w_bytes = {}
-        half = PACK // 2
 
-        def pick(g):
-            picked = sb("picked%d" % g, [P, PACK // PAIR, S], U32)
-            for u in range(PACK // PAIR):
-                n = PASSES * g + u
-                pairs = sb("x_pairs%d" % n, [P, T * PAIR], BF16, tag=["x_pairs", "x_pairs", "x_raw01", "x_grouped0"][n])
-                cut = X_ON_SCALAR[PASSES * g + u] // LINE
-                src = x_raw[g, u][:].rearrange("p e (c i) -> p c e i", i=LINE)
-                dst = pairs[:].rearrange("p (c i e) -> p c e i", i=LINE, e=PAIR)
-                if cut:
-                    nc.scalar.activation(out=dst[:, :cut], in_=src[:, :cut], func=COPY)
-                if cut < T // LINE:
-                    nc.vector.tensor_copy(out=dst[:, cut:], in_=src[:, cut:])
-                nc.vector.tensor_copy(out=picked[:, u, :], in_=pairs[:].bitcast(U32).indirect(offs_sb[:]))
-            return picked
+        picked = [sb("picked%d" % g, [P, PACK // PAIR, S], U32)[:] for g in range(PASSES)]
+
+        def as_pairs(rows, pairs):
+            return rows.rearrange("p e (c i) -> p c e i", i=LINE), pairs.rearrange("p (c i e) -> p c e i", i=LINE, e=PAIR)
+
+        def cast_x(n):
+            cut = X_ON_VECTOR[n] // LINE
+            src, dst = as_pairs(x_raw[n, 1][:], windows[n][:, T:])
+            nc.scalar.activation(out=dst, in_=src, func=COPY)
+            src, dst = as_pairs(x_raw[n, 0][:], windows[n][:, :T])
+            nc.scalar.activation(out=dst[:, cut:], in_=src[:, cut:], func=COPY)
+            if cut:
+                nc.vector.tensor_copy(out=dst[:, :cut], in_=src[:, :cut])
+
+        def pick(n, c0=0, c1=S):
+            g, u = divmod(n, 2)
+            nc.vector.tensor_copy(
+                out=picked[g][:, u, c0:c1], in_=windows[n].bitcast(U32).indirect(offs_sb[:, c0 // 16 : c1 // 16])
+            )
 
         def weave(grouped, picked):
             nc.vector.tensor_copy(
-                out=grouped.bitcast(I32).rearrange("p (c i u) -> p c u i", i=PAIR, u=PACK // PAIR),
-                in_=picked.bitcast(I32).rearrange("p u (c i) -> p c u i", i=PAIR),
+                out=grouped.bitcast(U32).rearrange("p (c i u) -> p c u i", i=PAIR, u=PACK // PAIR),
+                in_=picked.rearrange("p u (c i) -> p c u i", i=PAIR),
             )
 
-        def quantise(words, planes, values):
-            nc.vector.quantize_mx(out=words.bitcast(FP8X4), scales=planes, in_=values)
+        def quantise(name, values, width):
+            words = sb(name + "_words", [P, width], U32)
+            planes = sb(name + "_bytes", [P, width], U8)
+            nc.vector.quantize_mx(out=words[:].bitcast(FP8X4), scales=planes[:], in_=values)
+            return words, planes
 
-        def quantise_x(g, grouped, tag=None):
-            x_words[g] = sb("x_words%d" % g, [P, S], U32, tag=tag)
-            x_bytes[g] = sb("x_bytes%d" % g, [P, S], U8)
-            quantise(x_words[g][:], x_bytes[g][:], grouped)
+        def cast_w(a, g, values, on_scalar):
+            src = w_raw[a, g][:].rearrange("p j (c i) -> p c j i", i=LINE)
+            dst = values.rearrange("p (c i j) -> p c j i", i=LINE, j=PACK)
+            if on_scalar:
+                nc.scalar.activation(out=dst, in_=src, func=COPY)
+            else:
+                nc.vector.tensor_copy(out=dst, in_=src)
 
-        def w_tiles(name, keys):
-            words = sb("w_words" + name, [P, len(keys) * P], U32)
-            planes = sb("w_bytes" + name, [P, len(keys) * P], U8)
-            for n, key in enumerate(keys):
-                w_words[key] = words[:, n * P : (n + 1) * P]
-                w_bytes[key] = planes[:, n * P : (n + 1) * P]
-            return words[:], planes[:]
+        def quantise_w(a, g, values):
+            words, planes = quantise("w%d%d" % (a, g), values, HALF)
+            for n in range(2):
+                w_words[2 * a + n, g] = words[:, n * P : (n + 1) * P]
+                w_bytes[2 * a + n, g] = planes[:, n * P : (n + 1) * P]
 
-        def by_tile(values):
-            return values.rearrange("p (t m j) -> p m j t", t=half, j=PACK)
+        cast_x(0)
+        pick(0)
+        ratio = sb("ratio", [P, S], F32)
+        nc.scalar.activation(out=ratio[:], in_=ratio_bank[:], func=COPY)
+        cast_x(1)
+        pick(1)
+        grouped = sb("x_grouped0", [P, S * PACK], BF16)[:]
+        weave(grouped, picked[0])
+        x_words[0], x_bytes[0] = quantise("x0", grouped, S)
+        open_windows(1, "x_raw10")
+        cast_x(2)
+        pick(2)
+        cast_x(3)
+        pick(3, 0, S // 2)
+        pick(3, S // 2, S)
 
-        w_src = [w_raw[g][:].rearrange("p j (m t) -> p m j t", t=PACK) for g in range(PASSES)]
+        late = sb("late", [P, 3 * HALF * PACK], BF16, tag="x_raw31")
+        slots = [late[:, n * HALF * PACK : (n + 1) * HALF * PACK] for n in range(3)]
+        cast_w(0, 0, slots[0], True)
+        cast_w(0, 1, slots[1], True)
+        cast_w(1, 0, slots[2], True)
+        grouped = sb("x_grouped1", [P, S * PACK], BF16, tag="w_raw00")
+        x_words[1] = sb("x1_words", [P, S], U32)
+        x_bytes[1] = sb("x1_bytes", [P, S], U8)
 
-        grouped = sb("x_grouped0", [P, S * PACK], BF16)
-        weave(grouped[:], pick(0)[:])
-        quantise_x(0, grouped[:])
-        picked = pick(1)
+        def weave_half(a):
+            c0, c1 = a * (S // 2), (a + 1) * (S // 2)
+            weave(grouped[:, c0 * PACK : c1 * PACK], picked[1][:, :, c0:c1])
 
-        dealt = sb("w_dealt0", [P, S * PACK + half * K_PASS], BF16, tag="x_raw11")
-        early = dealt[:, : half * K_PASS]
-        late = dealt[:, S * PACK :]
-        nc.scalar.activation(out=by_tile(early), in_=w_src[0][:, :, :, :half], func=COPY)
-        nc.scalar.activation(out=by_tile(late), in_=w_src[0][:, :, :, half:], func=COPY)
-        quantise(*w_tiles("e0", [(0, 0), (1, 0)]), early)
-        weave(dealt[:, : S * PACK], picked[:])
-        quantise_x(1, dealt[:, : S * PACK])
-        quantise(*w_tiles("l0", [(2, 0), (3, 0)]), late)
+        def quantise_half(a):
+            c0, c1 = a * (S // 2), (a + 1) * (S // 2)
+            nc.vector.quantize_mx(
+                out=x_words[1][:, c0:c1].bitcast(FP8X4),
+                scales=x_bytes[1][:, c0:c1],
+                in_=grouped[:, c0 * PACK : c1 * PACK],
+            )
 
-        dealt = sb("w_dealt1", [P, PACK * K_PASS], BF16, tag="w_raw0")
-        early = dealt[:, : half * K_PASS]
-        late = dealt[:, half * K_PASS :]
-        nc.scalar.activation(out=by_tile(early), in_=w_src[1][:, :, :, :half], func=COPY)
-        nc.scalar.activation(out=by_tile(late), in_=w_src[1][:, :, :, half:], func=COPY)
-        for t in range(half):
-            quantise(*w_tiles("e1%d" % t, [(t, 1)]), early[:, t * K_PASS : (t + 1) * K_PASS])
-        quantise(*w_tiles("l1", [(2, 1), (3, 1)]), late)
+        weave_half(0)
+        quantise_w(0, 0, slots[0])
+        weave_half(1)
+        quantise_half(0)
+        quantise_w(0, 1, slots[1])
+        quantise_half(1)
+        cast_w(1, 1, slots[1], False)
+        quantise_w(1, 0, slots[2])
+        quantise_w(1, 1, slots[1])
 
-        partner = sb("partner", [P, PACK, S], F32)
-        for t in range(PACK):
-            pieces = [(0, 0, S // 2), (PACK, S // 2, S)] if t == 0 else [(t, 0, S)]
+        for t in range(TILES):
+            pieces = [(0, 0, S // 2), (2, S // 2, S)] if t == 0 else [([0, 1, 4, 5][t], 0, S)]
             accs = [bank(index) for index, c0, c1 in pieces]
             for g in range(PASSES):
                 for acc, (index, c0, c1) in zip(accs, pieces):
@@ -179,39 +241,74 @@ def tile_picked_mixup_gelu_e_kernel(
                     )
             for acc, (index, c0, c1) in zip(accs, pieces):
                 nc.scalar.activation(out=h[t][:, c0:c1], in_=acc[:, : c1 - c0], func=GELU)
-            nc.vector.tensor_tensor(out=partner[:, t, :], in0=h[t][:].indirect(pos_sb[:]), in1=mu_sb[:], op=MULT)
 
-        turned = []
-        for b in range(BLOCKS):
-            turned.append(bank(PACK + b))
-            for t in range(PACK):
-                nc.tensor.transpose(turned[b][:, t * P : (t + 1) * P], h[t][:, b * P : (b + 1) * P], ident[:])
-        own = []
-        for b in range(BLOCKS):
-            scaled = sb("scaled%d" % b, [P, S], F32)
-            nc.scalar.activation(out=scaled[:], in_=turned[b][:], func=COPY, scale=lam_cols[:, b : b + 1])
-            own.append(bank(b))
-            for t in range(PACK):
-                nc.tensor.transpose(own[b][:, t * P : (t + 1) * P], scaled[:, t * P : (t + 1) * P], ident[:])
+        def gather(t, c0, c1):
+            part = sb("partner%d_%d" % (t, c0), [P, c1 - c0], F32)
+            nc.vector.tensor_tensor(
+                out=part[:], in0=h[t][:].indirect(pos_sb[:, c0 // 16 : c1 // 16]), in1=ratio[:, c0:c1], op=MULT
+            )
+            return part
+
+        def turn_and_add(steps):
+            for n, (dst, src) in enumerate(steps):
+                nc.tensor.matmul(
+                    dst, lhsT=src, rhs=ident[:], is_transpose=True, start=(n == 0), stop=(n == len(steps) - 1)
+                )
+
+        turned = [sb("turned%d" % b, [P, H], BF16) for b in range(BLOCKS)]
+
+        def scale(b, a, summed):
+            nc.scalar.activation(
+                out=turned[b][:].rearrange("j (u a p e) -> j a u p e", u=PACK // PAIR, a=2, e=PAIR)[:, a],
+                in_=summed.rearrange("j (p u e) -> j u p e", u=PACK // PAIR, e=PAIR),
+                func=COPY,
+                scale=lam_cols[:, b : b + 1],
+            )
+
+        first = [gather(t, 0, S) for t in range(2)]
+        low = {}
+        for pair in range(2):
+            acc = bank(4 + pair)
+            blocks = [2 * pair, 2 * pair + 1]
+            steps = []
+            for source in (h, first):
+                for t in range(2):
+                    for b in blocks:
+                        c0 = (b % 2) * HALF + t * P
+                        steps.append((acc[:, c0 : c0 + P], source[t][:, b * P : (b + 1) * P]))
+            turn_and_add(steps)
+            for b in blocks:
+                low[b] = acc[:, (b % 2) * HALF : (b % 2 + 1) * HALF]
+
+        high = {}
+
+        def add_high(b):
+            second = [gather(t, b * P, (b + 1) * P) for t in (2, 3)]
+            high[b] = bank(b)
+            steps = [(high[b][:, n * P : (n + 1) * P], h[2 + n][:, b * P : (b + 1) * P]) for n in range(2)]
+            steps.extend((high[b][:, n * P : (n + 1) * P], second[n][:]) for n in range(2))
+            turn_and_add(steps)
+
+        def turn_back(b):
+            scale(b, 1, high[b][:, :HALF])
+            words = turned[b][:].bitcast(F32)
+            for u in range(PACK // PAIR):
+                nc.tensor.transpose(
+                    high[b][:, HALF + u * P : HALF + (u + 1) * P], words[:, u * P : (u + 1) * P], ident[:]
+                )
 
         out_rows = out.rearrange("(a m) j -> m a j", m=P)
-        z = [sb("z%d" % b, [P, P, PACK], BF16) for b in range(BLOCKS)]
 
-        def mix(b):
-            nc.vector.tensor_tensor(
-                out=z[b][:].rearrange("p (c i) t -> p c t i", i=PAIR),
-                in0=own[b][:].rearrange("p (t c i) -> p c t i", t=PACK, i=PAIR),
-                in1=partner[:, :, b * P : (b + 1) * P].rearrange("p t (c i) -> p c t i", i=PAIR),
-                op=ADD,
-            )
+        results = {}
 
         def finish(b):
-            z_words = sb("z_words%d" % b, [P, P], U32)
-            z_bytes = sb("z_bytes%d" % b, [P, P], U8)
-            nc.vector.quantize_mx(
-                out=z_words[:].bitcast(FP8X4), scales=z_bytes[:], in_=z[b][:].rearrange("p j t -> p (j t)")
+            z = sb("z%d" % b, [P, P * PACK], BF16)
+            (nc.vector.tensor_copy if b in (1, 2) else nc.scalar.copy)(
+                out=z[:].bitcast(F32).rearrange("p (j u) -> p j u", u=PACK // PAIR),
+                in_=high[b][:, HALF:].rearrange("p (u j) -> p j u", u=PACK // PAIR),
             )
-            res = bank(PACK + b)
+            z_words, z_bytes = quantise("z%d" % b, z[:], P)
+            res = bank([6, 7, 4, 5][b])
             for a in range(N // P):
                 nc.tensor.matmul_mx(
                     out=res[:, a * P : (a + 1) * P],
@@ -222,14 +319,28 @@ def tile_picked_mixup_gelu_e_kernel(
                     start=True,
                     stop=True,
                 )
+            results[b] = res
+
+        def store(b):
             staged = sb("staged%d" % b, [P, N], F32)
-            nc.scalar.activation(out=staged[:], in_=res[:, :N], func=COPY)
+            (nc.vector.tensor_copy if b % 2 else nc.scalar.copy)(out=staged[:], in_=results[b][:, :N])
             nc.sync.dma_start(
                 out=out_rows[:, :, b * P : (b + 1) * P], in_=staged[:].rearrange("p (a j) -> p a j", j=P)
             )
 
-        mix(0)
-        for b in range(1, BLOCKS):
-            mix(b)
-            finish(b - 1)
-        finish(BLOCKS - 1)
+        for b in range(BLOCKS):
+            add_high(b)
+        scale(0, 0, low[0])
+        scale(1, 0, low[1])
+        turn_back(0)
+        scale(2, 0, low[2])
+        turn_back(1)
+        scale(3, 0, low[3])
+        finish(0)
+        turn_back(2)
+        turn_back(3)
+        finish(1)
+        finish(2)
+        finish(3)
+        for b in range(BLOCKS):
+            store(b)

@@ -26,7 +26,7 @@ PACK = 4
 K_PASS = P * PACK
 PASSES = K // K_PASS
 PAIR = 2
-X_ON_VECTOR = [344, 344, 0, 344]
+X_ON_VECTOR = [344, 344, 0, 160]
 BLOCKS = S // P
 TILES = H // P
 HALF = H // 2
@@ -42,6 +42,7 @@ def tile_picked_mixup_gelu_e_kernel(
     nc = tc.nc
     with ExitStack() as ctx:
         keep = ctx.enter_context(tc.tile_pool(name="keep", bufs=1))
+        shared = ctx.enter_context(tc.tile_pool(name="shared", bufs=1))
         psum = ctx.enter_context(tc.psum_pool(name="psum", bufs=1))
 
         def sb(name, shape, dtype, tag=None):
@@ -56,7 +57,8 @@ def tile_picked_mixup_gelu_e_kernel(
         ident = sb("ident", [P, P], F32)
         share_rows = sb("share_rows", [P, P], F32)
         w2_bytes = sb("w2_bytes", [P, N], U8)
-        h = [sb("h%d" % t, [P, S + SPARE], F32) for t in range(TILES)]
+        h = {t: sb("h%d" % t, [P, S], F32) for t in (2, 3)}
+        zeros = sb("zeros", [P, 8], F32)
         warm = sb("warm", [P, 8], F32)
         loaded_rows = sb("loaded_rows", [2 * BLOCKS, P], F32)
         nc.sync.dma_start(out=loaded_rows[0:BLOCKS, :], in_=lam[0:1, :].rearrange("o (b j) -> (o b) j", j=P))
@@ -69,11 +71,10 @@ def tile_picked_mixup_gelu_e_kernel(
         nc.vector.scalar_tensor_tensor(
             out=share_rows[0 : 2 * BLOCKS, :], in0=floor[:], scalar=TINY, in1=loaded_rows[:], op0=ADD, op1=MAX
         )
-        for t in range(TILES):
-            nc.vector.memset(h[t][:, S:], 0.0)
+        nc.vector.memset(zeros[:], 0.0)
         make_identity(nc, ident[:])
         nc.vector.memset(w2_bytes[:].bitcast(I32), 0)
-        nc.scalar.activation(out=warm[:], in_=h[0][:, S:], func=GELU)
+        nc.scalar.activation(out=warm[:], in_=zeros[:], func=GELU)
 
         x_rows = xT.rearrange("(g p j) c -> g p j c", p=P, j=PACK)
         w_rows = w1.rearrange("(g p j) c -> g p j c", p=P, j=PACK)
@@ -91,7 +92,10 @@ def tile_picked_mixup_gelu_e_kernel(
                 nc.sync.dma_start(offs_sb[:], offs)
         for a in range(2):
             for g in range(PASSES):
-                w_raw[a, g] = sb("w_raw%d%d" % (a, g), [P, PACK, HALF], F32)
+                if (a, g) == (1, 0):
+                    w_raw[a, g] = shared.tile([P, PACK, HALF], F32, name="w_raw10", offset=0)
+                else:
+                    w_raw[a, g] = sb("w_raw%d%d" % (a, g), [P, PACK, HALF], F32)
                 nc.sync.dma_start(out=w_raw[a, g][:], in_=w_rows[g, :, :, a * HALF : (a + 1) * HALF])
             if a == 0:
                 nc.sync.dma_start(pos_sb[:], pos1)
@@ -197,7 +201,13 @@ def tile_picked_mixup_gelu_e_kernel(
         late = sb("late", [P, 3 * HALF * PACK], BF16, tag="x_raw31")
         slots = [late[:, n * HALF * PACK : (n + 1) * HALF * PACK] for n in range(3)]
         cast_w(0, 0, slots[0], True)
-        cast_w(0, 1, slots[1], True)
+        piece = P * PACK
+        for n in range(2):
+            nc.scalar.activation(
+                out=slots[1][:, n * piece : (n + 1) * piece].rearrange("p (c i j) -> p c j i", i=LINE, j=PACK),
+                in_=w_raw[0, 1][:, :, n * P : (n + 1) * P].rearrange("p j (c i) -> p c j i", i=LINE),
+                func=COPY,
+            )
         cast_w(1, 0, slots[2], True)
         grouped = sb("x_grouped1", [P, S * PACK], BF16, tag="w_raw00")
         x_words[1] = sb("x1_words", [P, S], U32)
@@ -215,16 +225,23 @@ def tile_picked_mixup_gelu_e_kernel(
                 in_=grouped[:, c0 * PACK : c1 * PACK],
             )
 
-        weave_half(0)
+        def quantise_tile(t, g, values):
+            words, planes = quantise("w_tile%d%d" % (t, g), values, P)
+            w_words[t, g], w_bytes[t, g] = words[:], planes[:]
+
         quantise_w(0, 0, slots[0])
+        weave_half(0)
         weave_half(1)
         quantise_half(0)
-        quantise_w(0, 1, slots[1])
+        quantise_tile(0, 1, slots[1][:, :piece])
         quantise_half(1)
+        quantise_tile(1, 1, slots[1][:, piece:])
         cast_w(1, 1, slots[1], False)
         quantise_w(1, 0, slots[2])
         quantise_w(1, 1, slots[1])
 
+        for t in range(2):
+            h[t] = shared.tile([P, S], F32, name="h%d" % t, offset=t * S * 4)
         for t in range(TILES):
             pieces = [(0, 0, S // 2), (2, S // 2, S)] if t == 0 else [([0, 1, 4, 5][t], 0, S)]
             accs = [bank(index) for index, c0, c1 in pieces]
@@ -242,11 +259,16 @@ def tile_picked_mixup_gelu_e_kernel(
             for acc, (index, c0, c1) in zip(accs, pieces):
                 nc.scalar.activation(out=h[t][:, c0:c1], in_=acc[:, : c1 - c0], func=GELU)
 
-        def gather(t, c0, c1):
-            part = sb("partner%d_%d" % (t, c0), [P, c1 - c0], F32)
-            nc.vector.tensor_tensor(
-                out=part[:], in0=h[t][:].indirect(pos_sb[:, c0 // 16 : c1 // 16]), in1=ratio[:, c0:c1], op=MULT
-            )
+        def gather(t, c0, c1, tag=None, pieces=1):
+            part = sb("partner%d_%d" % (t, c0), [P, c1 - c0], F32, tag=tag)
+            width = (c1 - c0) // pieces
+            for a in range(c0, c1, width):
+                nc.vector.tensor_tensor(
+                    out=part[:, a - c0 : a - c0 + width],
+                    in0=h[t][:].indirect(pos_sb[:, a // 16 : (a + width) // 16]),
+                    in1=ratio[:, a : a + width],
+                    op=MULT,
+                )
             return part
 
         def turn_and_add(steps):
@@ -265,10 +287,10 @@ def tile_picked_mixup_gelu_e_kernel(
                 scale=lam_cols[:, b : b + 1],
             )
 
-        first = [gather(t, 0, S) for t in range(2)]
+        first = [gather(0, 0, S, tag="w_raw11", pieces=2), gather(1, 0, S, pieces=2)]
         low = {}
         for pair in range(2):
-            acc = bank(4 + pair)
+            acc = bank([4, 7][pair])
             blocks = [2 * pair, 2 * pair + 1]
             steps = []
             for source in (h, first):
@@ -301,14 +323,22 @@ def tile_picked_mixup_gelu_e_kernel(
 
         results = {}
 
-        def finish(b):
-            z = sb("z%d" % b, [P, P * PACK], BF16)
-            (nc.vector.tensor_copy if b in (1, 2) else nc.scalar.copy)(
-                out=z[:].bitcast(F32).rearrange("p (j u) -> p j u", u=PACK // PAIR),
+        z = {}
+        z_mx = {}
+
+        def weave_z(b, copy):
+            z[b] = sb("z%d" % b, [P, P * PACK], BF16)
+            copy(
+                out=z[b][:].bitcast(F32).rearrange("p (j u) -> p j u", u=PACK // PAIR),
                 in_=high[b][:, HALF:].rearrange("p (u j) -> p j u", u=PACK // PAIR),
             )
-            z_words, z_bytes = quantise("z%d" % b, z[:], P)
-            res = bank([6, 7, 4, 5][b])
+
+        def quantise_z(b):
+            z_mx[b] = quantise("z%d" % b, z[b][:], P)
+
+        def finish(b):
+            z_words, z_bytes = z_mx[b]
+            res = bank([6, 5, 4, 7][b])
             for a in range(N // P):
                 nc.tensor.matmul_mx(
                     out=res[:, a * P : (a + 1) * P],
@@ -336,11 +366,14 @@ def tile_picked_mixup_gelu_e_kernel(
         scale(2, 0, low[2])
         turn_back(1)
         scale(3, 0, low[3])
-        finish(0)
         turn_back(2)
         turn_back(3)
-        finish(1)
-        finish(2)
-        finish(3)
+        weave_z(0, nc.vector.tensor_copy)
+        weave_z(1, nc.vector.tensor_copy)
+        weave_z(2, nc.vector.tensor_copy)
+        weave_z(3, nc.scalar.copy)
+        for b in range(BLOCKS):
+            quantise_z(b)
+            finish(b)
         for b in range(BLOCKS):
             store(b)

@@ -302,6 +302,18 @@ def tile_picked_mixup_gelu_e_kernel(
             for b in blocks:
                 low[b] = acc[:, (b % 2) * HALF : (b % 2 + 1) * HALF]
 
+        idle = bank(5)
+        for g in range(PASSES):
+            nc.tensor.matmul_mx(
+                out=idle[:],
+                lhsT=w_words[3, g].bitcast(FP8X4),
+                lhsT_scale=w_bytes[3, g],
+                rhs=x_words[g][:].bitcast(FP8X4),
+                rhs_scale=x_bytes[g][:],
+                start=True,
+                stop=True,
+            )
+
         high = {}
 
         def add_high(b):

@@ -93,12 +93,11 @@ def tile_picked_mixup_gelu_e_kernel(
         for a in range(2):
             for g in range(PASSES):
                 if (a, g) == (1, 0):
-                    w_raw[a, g] = shared.tile([P, PACK, HALF], F32, name="w_raw10", offset=0)
+                    w_raw[a, g] = shared.tile([P, PACK, HALF], F32, name="w_raw10", offset=0, align_bytes=64)
                 else:
                     w_raw[a, g] = sb("w_raw%d%d" % (a, g), [P, PACK, HALF], F32)
                 nc.sync.dma_start(out=w_raw[a, g][:], in_=w_rows[g, :, :, a * HALF : (a + 1) * HALF])
-            if a == 0:
-                nc.sync.dma_start(pos_sb[:], pos1)
+        nc.sync.dma_start(pos_sb[:], pos1)
         w2_codes = sb("w2_codes", [P, 2 * N], U8)
         nc.sync.dma_start(out=w2_codes[:].bitcast(I32), in_=w2_words[0].bitcast(I32))
         for q in range(4):
@@ -202,12 +201,17 @@ def tile_picked_mixup_gelu_e_kernel(
         slots = [late[:, n * HALF * PACK : (n + 1) * HALF * PACK] for n in range(3)]
         cast_w(0, 0, slots[0], True)
         piece = P * PACK
-        for n in range(2):
-            nc.scalar.activation(
-                out=slots[1][:, n * piece : (n + 1) * piece].rearrange("p (c i j) -> p c j i", i=LINE, j=PACK),
-                in_=w_raw[0, 1][:, :, n * P : (n + 1) * P].rearrange("p j (c i) -> p c j i", i=LINE),
-                func=COPY,
+
+        def as_words(t, values):
+            a, n = divmod(t, 2)
+            return (
+                w_raw[a, 1][:, :, n * P : (n + 1) * P].rearrange("p j (c i) -> p c j i", i=LINE),
+                values.rearrange("p (c i j) -> p c j i", i=LINE, j=PACK),
             )
+
+        for t in range(2):
+            src, dst = as_words(t, slots[1][:, t * piece : (t + 1) * piece])
+            nc.scalar.activation(out=dst, in_=src, func=COPY)
         cast_w(1, 0, slots[2], True)
         grouped = sb("x_grouped1", [P, S * PACK], BF16, tag="w_raw00")
         x_words[1] = sb("x1_words", [P, S], U32)
@@ -236,31 +240,33 @@ def tile_picked_mixup_gelu_e_kernel(
         quantise_tile(0, 1, slots[1][:, :piece])
         quantise_half(1)
         quantise_tile(1, 1, slots[1][:, piece:])
-        cast_w(1, 1, slots[1], False)
+        src, dst = as_words(2, slots[1][:, :piece])
+        nc.vector.tensor_copy(out=dst, in_=src)
         quantise_w(1, 0, slots[2])
-        quantise_w(1, 1, slots[1])
+        quantise_tile(2, 1, slots[1][:, :piece])
 
-        for t in range(2):
-            h[t] = shared.tile([P, S], F32, name="h%d" % t, offset=t * S * 4)
-        for t in range(TILES):
-            pieces = [(0, 0, S // 2), (2, S // 2, S)] if t == 0 else [([0, 1, 4, 5][t], 0, S)]
-            accs = [bank(index) for index, c0, c1 in pieces]
-            for g in range(PASSES):
-                for acc, (index, c0, c1) in zip(accs, pieces):
+        def product(t, pieces, order):
+            accs = [(bank(index)[:, : c1 - c0], c0, c1) for index, c0, c1 in pieces]
+            for g in order:
+                for acc, c0, c1 in accs:
                     nc.tensor.matmul_mx(
-                        out=acc[:, : c1 - c0],
+                        out=acc,
                         lhsT=w_words[t, g].bitcast(FP8X4),
                         lhsT_scale=w_bytes[t, g],
                         rhs=x_words[g][:, c0:c1].bitcast(FP8X4),
                         rhs_scale=x_bytes[g][:, c0:c1],
-                        start=(g == 0),
-                        stop=(g == PASSES - 1),
+                        start=(g == order[0]),
+                        stop=(g == order[-1]),
                     )
-            for acc, (index, c0, c1) in zip(accs, pieces):
-                nc.scalar.activation(out=h[t][:, c0:c1], in_=acc[:, : c1 - c0], func=GELU)
+            return accs
 
-        def gather(t, c0, c1, tag=None, pieces=1):
-            part = sb("partner%d_%d" % (t, c0), [P, c1 - c0], F32, tag=tag)
+        def gelu(t, accs):
+            for acc, c0, c1 in accs:
+                nc.scalar.activation(out=h[t][:, c0:c1], in_=acc, func=GELU)
+
+        def gather(t, c0, c1, part=None, pieces=1):
+            if part is None:
+                part = sb("partner%d_%d" % (t, c0), [P, c1 - c0], F32)[:]
             width = (c1 - c0) // pieces
             for a in range(c0, c1, width):
                 nc.vector.tensor_tensor(
@@ -270,6 +276,22 @@ def tile_picked_mixup_gelu_e_kernel(
                     op=MULT,
                 )
             return part
+
+        acc0 = product(0, [(0, 0, S // 2), (2, S // 2, S)], (0, 1))
+        acc1 = product(1, [(1, 0, S)], (0, 1))
+        acc2 = product(2, [(4, 0, S)], (0, 1))
+        h[0] = shared.tile([P, S], F32, name="h0", offset=0, align_bytes=64)
+        gelu(0, acc0)
+        fourth = shared.tile([P, piece], BF16, name="fourth", offset=S * 4, align_bytes=64)
+        src, dst = as_words(3, fourth[:])
+        nc.scalar.activation(out=dst, in_=src, func=COPY)
+        h[1] = sb("h1", [P, S], F32, tag="w_raw11")
+        gelu(1, acc1)
+        gelu(2, acc2)
+        first = [gather(0, 0, S, part=slots[2].bitcast(F32), pieces=2)]
+        quantise_tile(3, 1, fourth[:])
+        gelu(3, product(3, [(5, 0, S)], (1, 0)))
+        first.append(gather(1, 0, S, pieces=2))
 
         def turn_and_add(steps):
             for n, (dst, src) in enumerate(steps):
@@ -287,7 +309,6 @@ def tile_picked_mixup_gelu_e_kernel(
                 scale=lam_cols[:, b : b + 1],
             )
 
-        first = [gather(0, 0, S, tag="w_raw11", pieces=2), gather(1, 0, S, pieces=2)]
         low = {}
         for pair in range(2):
             acc = bank([4, 7][pair])
@@ -316,11 +337,16 @@ def tile_picked_mixup_gelu_e_kernel(
 
         high = {}
 
+        ahead = gather(2, 0, 2 * P)
+        late_parts = {(2, b): ahead[:, b * P : (b + 1) * P] for b in range(2)}
+        for t, b in [(3, 0), (3, 1), (2, 2), (3, 2), (2, 3), (3, 3)]:
+            late_parts[t, b] = gather(t, b * P, (b + 1) * P)
+
         def add_high(b):
-            second = [gather(t, b * P, (b + 1) * P) for t in (2, 3)]
+            second = [late_parts[t, b] for t in (2, 3)]
             high[b] = bank(b)
             steps = [(high[b][:, n * P : (n + 1) * P], h[2 + n][:, b * P : (b + 1) * P]) for n in range(2)]
-            steps.extend((high[b][:, n * P : (n + 1) * P], second[n][:]) for n in range(2))
+            steps.extend((high[b][:, n * P : (n + 1) * P], second[n]) for n in range(2))
             turn_and_add(steps)
 
         def turn_back(b):

@@ -23,15 +23,14 @@ MAX = mybir.AluOpType.max
 
 P = 128
 PACK = 4
-K_PASS = P * PACK
-PASSES = K // K_PASS
+PASSES = K // (P * PACK)
 PAIR = 2
-X_ON_VECTOR = [344, 344, 0, 160]
 BLOCKS = S // P
 TILES = H // P
 HALF = H // 2
-SPARE = 8
 LINE = 4
+EXTRA = 64
+H_AT = 512
 TINY = 2.0**-60
 HUGE = 2.0**120
 
@@ -46,6 +45,8 @@ def tile_picked_mixup_gelu_e_kernel(
         psum = ctx.enter_context(tc.psum_pool(name="psum", bufs=1))
 
         def sb(name, shape, dtype, tag=None):
+            if isinstance(tag, int):
+                return shared.tile(shape, dtype, name=name, offset=tag, align_bytes=64)
             return keep.tile(shape, dtype, name=name, tag=tag or name, align_bytes=64)
 
         def bank(index):
@@ -54,51 +55,28 @@ def tile_picked_mixup_gelu_e_kernel(
         offs_sb = keep.tile([P, S // 16], U16, name="offs_sb")
         pos_sb = keep.tile([P, S // 16], U16, name="pos_sb")
 
-        ident = sb("ident", [P, P], F32)
-        share_rows = sb("share_rows", [P, P], F32)
-        w2_bytes = sb("w2_bytes", [P, N], U8)
-        h = {t: sb("h%d" % t, [P, S], F32) for t in (2, 3)}
-        zeros = sb("zeros", [P, 8], F32)
-        warm = sb("warm", [P, 8], F32)
-        loaded_rows = sb("loaded_rows", [2 * BLOCKS, P], F32)
-        nc.sync.dma_start(out=loaded_rows[0:BLOCKS, :], in_=lam[0:1, :].rearrange("o (b j) -> (o b) j", j=P))
-        nc.sync.dma_start(out=loaded_rows[BLOCKS:, :], in_=mu[0:1, :].rearrange("o (b j) -> (o b) j", j=P))
-        nc.vector.memset(share_rows[:], 0.0)
-        floor = sb("floor", [2 * BLOCKS, P], F32)
-        nc.vector.tensor_scalar(
-            out=floor[:], in0=loaded_rows[:], scalar1=-TINY, scalar2=-HUGE, op0=IS_LE, op1=MULT
-        )
-        nc.vector.scalar_tensor_tensor(
-            out=share_rows[0 : 2 * BLOCKS, :], in0=floor[:], scalar=TINY, in1=loaded_rows[:], op0=ADD, op1=MAX
-        )
-        nc.vector.memset(zeros[:], 0.0)
-        make_identity(nc, ident[:])
-        nc.vector.memset(w2_bytes[:].bitcast(I32), 0)
-        nc.scalar.activation(out=warm[:], in_=zeros[:], func=GELU)
-
-        x_rows = xT.rearrange("(g p j) c -> g p j c", p=P, j=PACK)
+        x_rows = xT.rearrange("(g p j) c -> g j p c", p=P, j=PACK)
         w_rows = w1.rearrange("(g p j) c -> g p j c", p=P, j=PACK)
-        x_raw = {}
-        w_raw = {}
-        for n in range(2 * PASSES):
-            g, u = divmod(n, 2)
-            for a in (1, 0):
-                x_raw[n, a] = sb("x_raw%d%d" % (n, a), [P, PAIR, T // 2], F32)
-                nc.sync.dma_start(
-                    out=x_raw[n, a][:],
-                    in_=x_rows[g, :, PAIR * u : PAIR * (u + 1), a * (T // 2) : (a + 1) * (T // 2)],
-                )
+        loaded_rows = sb("loaded_rows", [2 * BLOCKS, P], F32)
+        x_raw = []
+        for n in range(PASSES * PACK):
+            x_raw.append(sb("x_raw%d" % n, [P, T], F32))
+            nc.sync.dma_start(out=x_raw[n][:], in_=x_rows[n // PACK, n % PACK])
             if n == 0:
                 nc.sync.dma_start(offs_sb[:], offs)
-        for a in range(2):
+                nc.sync.dma_start(out=loaded_rows[0:BLOCKS, :], in_=lam[0:1, :].rearrange("o (b j) -> (o b) j", j=P))
+                nc.sync.dma_start(out=loaded_rows[BLOCKS:, :], in_=mu[0:1, :].rearrange("o (b j) -> (o b) j", j=P))
+        w_raw = {}
+        w_both = {2: sb("w_both2", [P, PASSES, PACK, P], F32), 3: sb("w_both3", [P, PASSES, PACK, P], F32, H_AT)}
+        for t in range(TILES):
             for g in range(PASSES):
-                if (a, g) == (1, 0):
-                    w_raw[a, g] = shared.tile([P, PACK, HALF], F32, name="w_raw10", offset=0, align_bytes=64)
-                else:
-                    w_raw[a, g] = sb("w_raw%d%d" % (a, g), [P, PACK, HALF], F32)
-                nc.sync.dma_start(out=w_raw[a, g][:], in_=w_rows[g, :, :, a * HALF : (a + 1) * HALF])
-        nc.sync.dma_start(pos_sb[:], pos1)
+                w_raw[t, g] = w_both[t][:, g] if t in w_both else sb("w_raw%d%d" % (t, g), [P, PACK, P], F32)[:]
+                nc.sync.dma_start(out=w_raw[t, g], in_=w_rows[g, :, :, t * P : (t + 1) * P])
+            if t == 1:
+                nc.sync.dma_start(pos_sb[:], pos1)
         w2_codes = sb("w2_codes", [P, 2 * N], U8)
+        w2_bytes = sb("w2_bytes", [P, N], U8)
+        nc.vector.memset(w2_bytes[:].bitcast(I32), 0)
         nc.sync.dma_start(out=w2_codes[:].bitcast(I32), in_=w2_words[0].bitcast(I32))
         for q in range(4):
             nc.sync.dma_start(
@@ -106,280 +84,265 @@ def tile_picked_mixup_gelu_e_kernel(
                 in_=w2_scales[0, 4 * q : 4 * q + 4, :].bitcast(I32),
             )
 
+        ident = sb("ident", [P, P], F32)
+        share_rows = sb("share_rows", [P, P], F32)
+        zeros = sb("zeros", [P, 8], F32)
+        warm = sb("warm", [P, 8], F32)
+        nc.vector.memset(zeros[:], 0.0)
+        nc.vector.memset(share_rows[:], 0.0)
+        make_identity(nc, ident[:])
+        nc.scalar.activation(out=warm[:], in_=zeros[:], func=GELU)
+
+        floor = sb("floor", [2 * BLOCKS, P], F32)
+        nc.vector.tensor_scalar(
+            out=floor[:], in0=loaded_rows[:], scalar1=-TINY, scalar2=-HUGE, op0=IS_LE, op1=MULT
+        )
+        nc.vector.scalar_tensor_tensor(
+            out=share_rows[0 : 2 * BLOCKS, :], in0=floor[:], scalar=TINY, in1=loaded_rows[:], op0=ADD, op1=MAX
+        )
         share_bank = bank(6)
         nc.tensor.transpose(share_bank[:, 0:P], share_rows[:], ident[:])
-        lam_given = share_bank[:, 0:BLOCKS]
-        mu_given = share_bank[:, BLOCKS : 2 * BLOCKS]
         lam_cols = sb("lam_cols", [P, BLOCKS], F32)
-        windows = {}
-
-        def open_windows(g, tag=None):
-            both = sb("x_pairs%d" % g, [P, (2 * T - SPARE) * PAIR], BF16, tag=tag)
-            for u in range(2):
-                windows[2 * g + u] = both[:, u * (T - SPARE) * PAIR : (u * (T - SPARE) + T) * PAIR]
-
-        open_windows(0)
-        inverse = windows[0].bitcast(F32)[:, :BLOCKS]
+        planes = [sb("planes%d" % g, [P, PACK, S], BF16) for g in range(PASSES)]
+        inverse = planes[0][:, PACK - 1, : 2 * BLOCKS].bitcast(F32)
         ratio_cols = sb("ratio_cols", [P, BLOCKS], F32)
-        nc.vector.reciprocal(out=inverse, in_=lam_given)
-        nc.vector.tensor_tensor(out=ratio_cols[:], in0=mu_given, in1=inverse, op=MULT)
-        nc.vector.tensor_copy(out=lam_cols[:], in_=lam_given)
+        nc.vector.reciprocal(out=inverse, in_=share_bank[:, 0:BLOCKS])
+        nc.vector.tensor_copy(out=lam_cols[:], in_=share_bank[:, 0:BLOCKS])
+        nc.vector.tensor_tensor(out=ratio_cols[:], in0=share_bank[:, BLOCKS : 2 * BLOCKS], in1=inverse, op=MULT)
         ratio_bank = bank(7)
         for b in range(BLOCKS):
             nc.tensor.transpose(
                 ratio_bank[:, b * P : (b + 1) * P], ratio_cols[:, b : b + 1].to_broadcast([P, P]), ident[:]
             )
+        ratio = sb("ratio", [P, S], F32)
+        nc.vector.tensor_copy(out=ratio[:], in_=ratio_bank[:])
 
-        x_words = {}
-        x_bytes = {}
-        w_words = {}
-        w_bytes = {}
-
-        picked = [sb("picked%d" % g, [P, PACK // PAIR, S], U32)[:] for g in range(PASSES)]
-
-        def as_pairs(rows, pairs):
-            return rows.rearrange("p e (c i) -> p c e i", i=LINE), pairs.rearrange("p (c i e) -> p c e i", i=LINE, e=PAIR)
-
-        def cast_x(n):
-            cut = X_ON_VECTOR[n] // LINE
-            src, dst = as_pairs(x_raw[n, 1][:], windows[n][:, T:])
-            nc.scalar.activation(out=dst, in_=src, func=COPY)
-            src, dst = as_pairs(x_raw[n, 0][:], windows[n][:, :T])
-            nc.scalar.activation(out=dst[:, cut:], in_=src[:, cut:], func=COPY)
-            if cut:
-                nc.vector.tensor_copy(out=dst[:, :cut], in_=src[:, :cut])
-
-        def pick(n, c0=0, c1=S):
-            g, u = divmod(n, 2)
-            nc.vector.tensor_copy(
-                out=picked[g][:, u, c0:c1], in_=windows[n].bitcast(U32).indirect(offs_sb[:, c0 // 16 : c1 // 16])
-            )
-
-        def weave(grouped, picked):
-            nc.vector.tensor_copy(
-                out=grouped.bitcast(U32).rearrange("p (c i u) -> p c u i", i=PAIR, u=PACK // PAIR),
-                in_=picked.rearrange("p u (c i) -> p c u i", i=PAIR),
-            )
-
-        def quantise(name, values, width):
-            words = sb(name + "_words", [P, width], U32)
-            planes = sb(name + "_bytes", [P, width], U8)
-            nc.vector.quantize_mx(out=words[:].bitcast(FP8X4), scales=planes[:], in_=values)
-            return words, planes
-
-        def cast_w(a, g, values, on_scalar):
-            src = w_raw[a, g][:].rearrange("p j (c i) -> p c j i", i=LINE)
-            dst = values.rearrange("p (c i j) -> p c j i", i=LINE, j=PACK)
+        def move(on_scalar, dst, src):
             if on_scalar:
                 nc.scalar.activation(out=dst, in_=src, func=COPY)
             else:
                 nc.vector.tensor_copy(out=dst, in_=src)
 
-        def quantise_w(a, g, values):
-            words, planes = quantise("w%d%d" % (a, g), values, HALF)
-            for n in range(2):
-                w_words[2 * a + n, g] = words[:, n * P : (n + 1) * P]
-                w_bytes[2 * a + n, g] = planes[:, n * P : (n + 1) * P]
+        def pick(n, on_scalar, c0=0, c1=S):
+            move(on_scalar, planes[n // PACK][:, n % PACK, c0:c1], x_raw[n][:].indirect(offs_sb[:, c0 // 16 : c1 // 16]))
 
-        cast_x(0)
-        pick(0)
-        ratio = sb("ratio", [P, S], F32)
-        nc.scalar.activation(out=ratio[:], in_=ratio_bank[:], func=COPY)
-        cast_x(1)
-        pick(1)
-        grouped = sb("x_grouped0", [P, S * PACK], BF16)[:]
-        weave(grouped, picked[0])
-        x_words[0], x_bytes[0] = quantise("x0", grouped, S)
-        open_windows(1, "x_raw10")
-        cast_x(2)
-        pick(2)
-        cast_x(3)
-        pick(3, 0, S // 2)
-        pick(3, S // 2, S)
+        def weave(on_scalar, grouped, rows):
+            move(
+                on_scalar,
+                grouped.rearrange("p (c i j) -> p c j i", i=LINE, j=PACK),
+                rows.rearrange("p j (c i) -> p c j i", i=LINE),
+            )
 
-        late = sb("late", [P, 3 * HALF * PACK], BF16, tag="x_raw31")
-        slots = [late[:, n * HALF * PACK : (n + 1) * HALF * PACK] for n in range(3)]
-        cast_w(0, 0, slots[0], True)
+        def quantise(words, scale_bytes, values):
+            nc.vector.quantize_mx(out=words.bitcast(FP8X4), scales=scale_bytes, in_=values)
+
+        x_grouped = [sb("x_grouped%d" % g, [P, S * PACK], BF16) for g in range(PASSES)]
+        x_words = {0: sb("x_words0", [P, S], U32)}
+        x_bytes = [sb("x_bytes%d" % g, [P, S], U8) for g in range(PASSES)]
+
+        def weave_pair(g, u, c0, c1):
+            words = x_grouped[g][:, c0 * PACK : c1 * PACK].rearrange("p (c i u e) -> p u c e i", i=LINE, u=PACK // PAIR, e=PAIR)
+            rows = planes[g][:, PAIR * u : PAIR * (u + 1), c0:c1].rearrange("p e (c i) -> p c e i", i=LINE)
+            nc.vector.tensor_copy(out=words[:, u], in_=rows)
+
+        def quantise_x(g, c0, c1):
+            quantise(x_words[g][:, c0:c1], x_bytes[g][:, c0:c1], x_grouped[g][:, c0 * PACK : c1 * PACK])
+
+        for n in range(PACK - 1):
+            pick(n, n % 2 == 0)
+        pick(3, False, 0, S // 2)
+        pick(3, True, S // 2, S)
+        weave(False, x_grouped[0][:], planes[0][:])
+        pick(4, True)
+        quantise_x(0, 0, S)
+        pick(5, True)
+        weave_pair(1, 0, 0, S)
+        pick(6, True)
+        pick(7, False, 0, P)
+        pick(7, False, P, 2 * P + EXTRA)
+        pick(7, True, 2 * P + EXTRA, S)
+
         piece = P * PACK
+        w_grouped = [sb("w_grouped%d" % t, [P, PASSES * piece], BF16) for t in range(TILES)]
+        w_words = {}
+        w_bytes = {}
 
-        def as_words(t, values):
-            a, n = divmod(t, 2)
-            return (
-                w_raw[a, 1][:, :, n * P : (n + 1) * P].rearrange("p j (c i) -> p c j i", i=LINE),
-                values.rearrange("p (c i j) -> p c j i", i=LINE, j=PACK),
+        def round_w(on_scalar, t, g):
+            weave(on_scalar, w_grouped[t][:, g * piece : (g + 1) * piece], w_raw[t, g])
+
+        def quantise_w(t, g0, g1):
+            words = sb("w_words%d%d" % (t, g0), [P, (g1 - g0) * P], U32)
+            scale_bytes = sb("w_bytes%d%d" % (t, g0), [P, (g1 - g0) * P], U8)
+            quantise(words[:], scale_bytes[:], w_grouped[t][:, g0 * piece : g1 * piece])
+            for g in range(g0, g1):
+                w_words[t, g] = words[:, (g - g0) * P : (g - g0 + 1) * P]
+                w_bytes[t, g] = scale_bytes[:, (g - g0) * P : (g - g0 + 1) * P]
+
+        acc = {}
+
+        def multiply(dst, t, g, c0, c1, start, stop):
+            nc.tensor.matmul_mx(
+                out=dst[:, c0:c1],
+                lhsT=w_words[t, g].bitcast(FP8X4),
+                lhsT_scale=w_bytes[t, g],
+                rhs=x_words[g][:, c0:c1].bitcast(FP8X4),
+                rhs_scale=x_bytes[g][:, c0:c1],
+                start=start,
+                stop=stop,
             )
 
-        for t in range(2):
-            src, dst = as_words(t, slots[1][:, t * piece : (t + 1) * piece])
-            nc.scalar.activation(out=dst, in_=src, func=COPY)
-        cast_w(1, 0, slots[2], True)
-        grouped = sb("x_grouped1", [P, S * PACK], BF16, tag="w_raw00")
-        x_words[1] = sb("x1_words", [P, S], U32)
-        x_bytes[1] = sb("x1_bytes", [P, S], U8)
+        def product(t):
+            acc[t] = bank(t)
+            for g in range(PASSES):
+                multiply(acc[t], t, g, 0, S, g == 0, g == PASSES - 1)
 
-        def weave_half(a):
-            c0, c1 = a * (S // 2), (a + 1) * (S // 2)
-            weave(grouped[:, c0 * PACK : c1 * PACK], picked[1][:, :, c0:c1])
+        h = {}
+        fetched = {}
 
-        def quantise_half(a):
-            c0, c1 = a * (S // 2), (a + 1) * (S // 2)
-            nc.vector.quantize_mx(
-                out=x_words[1][:, c0:c1].bitcast(FP8X4),
-                scales=x_bytes[1][:, c0:c1],
-                in_=grouped[:, c0 * PACK : c1 * PACK],
-            )
+        def gelu(t, tag=None):
+            h[t] = sb("h%d" % t, [P, S], F32, tag)
+            nc.scalar.activation(out=h[t][:], in_=acc[t][:], func=GELU)
 
-        def quantise_tile(t, g, values):
-            words, planes = quantise("w_tile%d%d" % (t, g), values, P)
-            w_words[t, g], w_bytes[t, g] = words[:], planes[:]
+        def fetch(t, c0, c1, tag=None):
+            fetched[t, c0] = sb("fetched%d_%d" % (t, c0), [P, c1 - c0], F32, tag)
+            move(True, fetched[t, c0][:], h[t][:].indirect(pos_sb[:, c0 // 16 : c1 // 16]))
 
-        quantise_w(0, 0, slots[0])
-        weave_half(0)
-        weave_half(1)
-        quantise_half(0)
-        quantise_tile(0, 1, slots[1][:, :piece])
-        quantise_half(1)
-        quantise_tile(1, 1, slots[1][:, piece:])
-        src, dst = as_words(2, slots[1][:, :piece])
-        nc.vector.tensor_copy(out=dst, in_=src)
-        quantise_w(1, 0, slots[2])
-        quantise_tile(2, 1, slots[1][:, :piece])
+        mid = S // 2
+        for t, g in [(0, 0), (0, 1), (1, 0), (1, 1)]:
+            round_w(True, t, g)
+        for c0, c1 in [(0, P), (P, mid), (mid, S)]:
+            weave_pair(1, 1, c0, c1)
+        quantise_w(0, 0, 1)
+        quantise_w(0, 1, 2)
+        x_words[1] = sb("x_words1", [P, S], U32, "w_raw01")
+        pieces = [(bank(0), 0, mid), (bank(4), mid, mid + P), (bank(5), mid + P, S)]
+        for half, c0, c1 in pieces:
+            quantise_x(1, c0, c1)
+        h[0] = sb("h0", [P, S], F32, "w_raw11")
+        for g in range(PASSES):
+            for half, c0, c1 in pieces:
+                multiply(half, 0, g, c0, c1, g == 0, g == PASSES - 1)
+        for half, c0, c1 in pieces:
+            nc.scalar.activation(out=h[0][:, c0:c1], in_=half[:, c0:c1], func=GELU)
+        quantise_w(1, 0, PASSES)
+        product(1)
+        nc.vector.tensor_copy(
+            out=w_grouped[2][:].rearrange("p (g c i j) -> p g c j i", g=PASSES, i=LINE, j=PACK),
+            in_=w_both[2][:].rearrange("p g j (c i) -> p g c j i", i=LINE),
+        )
+        quantise_w(2, 0, PASSES)
+        product(2)
+        round_w(True, 3, 0)
+        round_w(True, 3, 1)
+        gelu(1, 2 * H_AT)
+        gelu(2, 2 * H_AT + S * 4)
 
-        def product(t, pieces, order):
-            accs = [(bank(index)[:, : c1 - c0], c0, c1) for index, c0, c1 in pieces]
-            for g in order:
-                for acc, c0, c1 in accs:
-                    nc.tensor.matmul_mx(
-                        out=acc,
-                        lhsT=w_words[t, g].bitcast(FP8X4),
-                        lhsT_scale=w_bytes[t, g],
-                        rhs=x_words[g][:, c0:c1].bitcast(FP8X4),
-                        rhs_scale=x_bytes[g][:, c0:c1],
-                        start=(g == order[0]),
-                        stop=(g == order[-1]),
-                    )
-            return accs
+        partner = {}
 
-        def gelu(t, accs):
-            for acc, c0, c1 in accs:
-                nc.scalar.activation(out=h[t][:, c0:c1], in_=acc, func=GELU)
-
-        def gather(t, c0, c1, part=None, pieces=1):
-            if part is None:
-                part = sb("partner%d_%d" % (t, c0), [P, c1 - c0], F32)[:]
-            width = (c1 - c0) // pieces
-            for a in range(c0, c1, width):
-                nc.vector.tensor_tensor(
-                    out=part[:, a - c0 : a - c0 + width],
-                    in0=h[t][:].indirect(pos_sb[:, a // 16 : (a + width) // 16]),
-                    in1=ratio[:, a : a + width],
-                    op=MULT,
-                )
+        def place(t, c0, c1, tag):
+            part = sb("term%d_%d" % (t, c0), [P, c1 - c0], F32, tag)[:]
+            for b in range(c0 // P, c1 // P):
+                partner[t, b] = part[:, b * P - c0 : (b + 1) * P - c0]
             return part
 
-        acc0 = product(0, [(0, 0, S // 2), (2, S // 2, S)], (0, 1))
-        acc1 = product(1, [(1, 0, S)], (0, 1))
-        acc2 = product(2, [(4, 0, S)], (0, 1))
-        h[0] = shared.tile([P, S], F32, name="h0", offset=0, align_bytes=64)
-        gelu(0, acc0)
-        fourth = shared.tile([P, piece], BF16, name="fourth", offset=S * 4, align_bytes=64)
-        src, dst = as_words(3, fourth[:])
-        nc.scalar.activation(out=dst, in_=src, func=COPY)
-        h[1] = sb("h1", [P, S], F32, tag="w_raw11")
-        gelu(1, acc1)
-        gelu(2, acc2)
-        first = [gather(0, 0, S, part=slots[2].bitcast(F32), pieces=2)]
-        quantise_tile(3, 1, fourth[:])
-        gelu(3, product(3, [(5, 0, S)], (1, 0)))
-        first.append(gather(1, 0, S, pieces=2))
+        def gather(t, c0, c1, tag=None):
+            nc.vector.tensor_tensor(
+                out=place(t, c0, c1, tag),
+                in0=h[t][:].indirect(pos_sb[:, c0 // 16 : c1 // 16]),
+                in1=ratio[:, c0:c1],
+                op=MULT,
+            )
 
-        def turn_and_add(steps):
-            for n, (dst, src) in enumerate(steps):
-                nc.tensor.matmul(
-                    dst, lhsT=src, rhs=ident[:], is_transpose=True, start=(n == 0), stop=(n == len(steps) - 1)
-                )
+        def weigh(t, c0, c1):
+            nc.vector.tensor_tensor(out=place(t, c0, c1, None), in0=fetched[t, c0][:], in1=ratio[:, c0:c1], op=MULT)
+
+        last = TILES - 1
+        early = [bank(index) for index in (5, 6, 7, 0)]
+        apart = [bank(index) for index in (4, 1)]
+        left = {}
+
+        def home(t, b):
+            if t < last:
+                return ("early", b), early[b][:, t * P : (t + 1) * P], 2 * last
+            return ("apart", b // 2), apart[b // 2][:, (b % 2) * P : (b % 2 + 1) * P], 4
+
+        def turn(t, b, src):
+            group, dst, size = home(t, b)
+            left[group] = left.get(group, size) - 1
+            nc.tensor.matmul(
+                dst, lhsT=src, rhs=ident[:], is_transpose=True, start=(left[group] == size - 1), stop=(left[group] == 0)
+            )
+
+        def turn_partner(t, c0, c1):
+            for b in range(c0 // P, c1 // P):
+                turn(t, b, partner[t, b])
+
+        def turn_own(t, c0, c1):
+            for b in range(c0 // P, c1 // P):
+                turn(t, b, h[t][:, b * P : (b + 1) * P])
 
         turned = [sb("turned%d" % b, [P, H], BF16) for b in range(BLOCKS)]
 
-        def scale(b, a, summed):
-            nc.scalar.activation(
-                out=turned[b][:].rearrange("j (u a p e) -> j a u p e", u=PACK // PAIR, a=2, e=PAIR)[:, a],
-                in_=summed.rearrange("j (p u e) -> j u p e", u=PACK // PAIR, e=PAIR),
-                func=COPY,
-                scale=lam_cols[:, b : b + 1],
-            )
+        def scale(on_scalar, b, t0, t1):
+            dst = turned[b][:].rearrange("j (u l e) -> j u l e", u=PACK // PAIR, e=PAIR)[:, :, t0 * 32 : t1 * 32]
+            src = early[b][:, : last * P] if t0 == 0 else home(last, b)[1]
+            src = src.rearrange("j (l u e) -> j u l e", u=PACK // PAIR, e=PAIR)
+            if on_scalar:
+                nc.scalar.activation(out=dst, in_=src, func=COPY, scale=lam_cols[:, b : b + 1])
+            else:
+                nc.vector.tensor_scalar(out=dst, in0=src, scalar1=lam_cols[:, b : b + 1], scalar2=None, op0=MULT)
 
-        low = {}
-        for pair in range(2):
-            acc = bank([4, 7][pair])
-            blocks = [2 * pair, 2 * pair + 1]
-            steps = []
-            for source in (h, first):
-                for t in range(2):
-                    for b in blocks:
-                        c0 = (b % 2) * HALF + t * P
-                        steps.append((acc[:, c0 : c0 + P], source[t][:, b * P : (b + 1) * P]))
-            turn_and_add(steps)
-            for b in blocks:
-                low[b] = acc[:, (b % 2) * HALF : (b % 2 + 1) * HALF]
+        back = {}
 
-        idle = bank(5)
-        for g in range(PASSES):
-            nc.tensor.matmul_mx(
-                out=idle[:],
-                lhsT=w_words[3, g].bitcast(FP8X4),
-                lhsT_scale=w_bytes[3, g],
-                rhs=x_words[g][:].bitcast(FP8X4),
-                rhs_scale=x_bytes[g][:],
-                start=True,
-                stop=True,
-            )
-
-        high = {}
-
-        ahead = gather(2, 0, 2 * P)
-        late_parts = {(2, b): ahead[:, b * P : (b + 1) * P] for b in range(2)}
-        for t, b in [(3, 0), (3, 1), (2, 2), (3, 2), (2, 3), (3, 3)]:
-            late_parts[t, b] = gather(t, b * P, (b + 1) * P)
-
-        def add_high(b):
-            second = [late_parts[t, b] for t in (2, 3)]
-            high[b] = bank(b)
-            steps = [(high[b][:, n * P : (n + 1) * P], h[2 + n][:, b * P : (b + 1) * P]) for n in range(2)]
-            steps.extend((high[b][:, n * P : (n + 1) * P], second[n]) for n in range(2))
-            turn_and_add(steps)
-
-        def turn_back(b):
-            scale(b, 1, high[b][:, :HALF])
+        def turn_back(b, dst):
+            back[b] = dst
             words = turned[b][:].bitcast(F32)
             for u in range(PACK // PAIR):
-                nc.tensor.transpose(
-                    high[b][:, HALF + u * P : HALF + (u + 1) * P], words[:, u * P : (u + 1) * P], ident[:]
-                )
+                nc.tensor.transpose(dst[:, u * P : (u + 1) * P], words[:, u * P : (u + 1) * P], ident[:])
+
+        turn_own(0, 0, S)
+        gather(0, 0, mid, "w_both2")
+        turn_partner(0, 0, mid)
+        quantise_w(3, 0, PASSES)
+        product(3)
+        gelu(3)
+        fetch(3, 0, mid)
+        fetch(3, mid, S)
+        gather(0, mid, S, 0)
+        turn_partner(0, mid, S)
+        turn_own(1, 0, S)
+        gather(1, 0, mid)
+        turn_partner(1, 0, mid)
+        turn_own(2, 0, S)
+        gather(1, mid, S)
+        turn_partner(1, mid, S)
+        turn_own(3, 0, S)
+        for c0, c1 in [(0, mid), (mid, S)]:
+            gather(2, c0, c1)
+            turn_partner(2, c0, c1)
+        for c0, c1 in [(0, mid), (mid, S)]:
+            weigh(3, c0, c1)
+            turn_partner(3, c0, c1)
 
         out_rows = out.rearrange("(a m) j -> m a j", m=P)
-
         results = {}
-
         z = {}
-        z_mx = {}
 
         def weave_z(b, copy):
             z[b] = sb("z%d" % b, [P, P * PACK], BF16)
             copy(
                 out=z[b][:].bitcast(F32).rearrange("p (j u) -> p j u", u=PACK // PAIR),
-                in_=high[b][:, HALF:].rearrange("p (u j) -> p j u", u=PACK // PAIR),
+                in_=back[b].rearrange("p (u j) -> p j u", u=PACK // PAIR),
             )
 
-        def quantise_z(b):
-            z_mx[b] = quantise("z%d" % b, z[b][:], P)
-
         def finish(b):
-            z_words, z_bytes = z_mx[b]
-            res = bank([6, 5, 4, 7][b])
+            z_words = sb("z_words%d" % b, [P, P], U32)
+            z_bytes = sb("z_bytes%d" % b, [P, P], U8)
+            quantise(z_words[:], z_bytes[:], z[b][:])
+            results[b] = bank([5, 6, 7, 0][b])
             for a in range(N // P):
                 nc.tensor.matmul_mx(
-                    out=res[:, a * P : (a + 1) * P],
+                    out=results[b][:, a * P : (a + 1) * P],
                     lhsT=w2_codes[:, 2 * a * P : 2 * (a + 1) * P].bitcast(FP4X4),
                     lhsT_scale=w2_bytes[:, a * P : (a + 1) * P],
                     rhs=z_words[:].bitcast(FP8X4),
@@ -387,31 +350,23 @@ def tile_picked_mixup_gelu_e_kernel(
                     start=True,
                     stop=True,
                 )
-            results[b] = res
 
-        def store(b):
+        def store(b, copy):
             staged = sb("staged%d" % b, [P, N], F32)
-            (nc.vector.tensor_copy if b % 2 else nc.scalar.copy)(out=staged[:], in_=results[b][:, :N])
+            copy(out=staged[:], in_=results[b][:, :N])
             nc.sync.dma_start(
                 out=out_rows[:, :, b * P : (b + 1) * P], in_=staged[:].rearrange("p (a j) -> p a j", j=P)
             )
 
         for b in range(BLOCKS):
-            add_high(b)
-        scale(0, 0, low[0])
-        scale(1, 0, low[1])
-        turn_back(0)
-        scale(2, 0, low[2])
-        turn_back(1)
-        scale(3, 0, low[3])
-        turn_back(2)
-        turn_back(3)
-        weave_z(0, nc.vector.tensor_copy)
-        weave_z(1, nc.vector.tensor_copy)
-        weave_z(2, nc.vector.tensor_copy)
-        weave_z(3, nc.scalar.copy)
+            scale(True, b, 0, last)
         for b in range(BLOCKS):
-            quantise_z(b)
+            scale(False, b, last, TILES)
+        for b, dst in enumerate([apart[0][:, HALF:], bank(2)[:, :HALF], apart[1][:, HALF:], bank(3)[:, :HALF]]):
+            turn_back(b, dst)
+        for b in range(BLOCKS):
+            weave_z(b, nc.scalar.copy if b % 2 else nc.vector.tensor_copy)
+        for b in range(BLOCKS):
             finish(b)
         for b in range(BLOCKS):
-            store(b)
+            store(b, nc.vector.tensor_copy if b % 2 else nc.scalar.copy)

@@ -30,7 +30,7 @@ TILES = H // P
 HALF = H // 2
 LINE = 4
 EXTRA = 64
-H_AT = 512
+LAST_AT = (1024, 8192)
 TINY = 2.0**-60
 HUGE = 2.0**120
 
@@ -67,10 +67,10 @@ def tile_picked_mixup_gelu_e_kernel(
                 nc.sync.dma_start(out=loaded_rows[0:BLOCKS, :], in_=lam[0:1, :].rearrange("o (b j) -> (o b) j", j=P))
                 nc.sync.dma_start(out=loaded_rows[BLOCKS:, :], in_=mu[0:1, :].rearrange("o (b j) -> (o b) j", j=P))
         w_raw = {}
-        w_both = {2: sb("w_both2", [P, PASSES, PACK, P], F32), 3: sb("w_both3", [P, PASSES, PACK, P], F32, H_AT)}
+        w_both = {2: sb("w_both2", [P, PASSES, PACK, P], F32)}
         for t in range(TILES):
             for g in range(PASSES):
-                w_raw[t, g] = w_both[t][:, g] if t in w_both else sb("w_raw%d%d" % (t, g), [P, PACK, P], F32)[:]
+                w_raw[t, g] = w_both[t][:, g] if t in w_both else sb("w_raw%d%d" % (t, g), [P, PACK, P], F32, LAST_AT[g] if t == 3 else None)[:]
                 nc.sync.dma_start(out=w_raw[t, g], in_=w_rows[g, :, :, t * P : (t + 1) * P])
             if t == 1:
                 nc.sync.dma_start(pos_sb[:], pos1)
@@ -233,9 +233,12 @@ def tile_picked_mixup_gelu_e_kernel(
         quantise_w(2, 0, PASSES)
         product(2)
         round_w(True, 3, 0)
+        quantise_w(3, 0, 1)
+        acc[3] = bank(3)
+        multiply(acc[3], 3, 0, 0, S, True, False)
+        gelu(1, 0)
         round_w(True, 3, 1)
-        gelu(1, 2 * H_AT)
-        gelu(2, 2 * H_AT + S * 4)
+        gelu(2, 6656)
 
         partner = {}
 
@@ -303,18 +306,18 @@ def tile_picked_mixup_gelu_e_kernel(
         turn_own(0, 0, S)
         gather(0, 0, mid, "w_both2")
         turn_partner(0, 0, mid)
-        quantise_w(3, 0, PASSES)
-        product(3)
+        quantise_w(3, 1, PASSES)
+        multiply(acc[3], 3, 1, 0, S, False, True)
         gelu(3)
         fetch(3, 0, mid)
         fetch(3, mid, S)
-        gather(0, mid, S, 0)
+        gather(0, mid, S, 2048)
         turn_partner(0, mid, S)
         turn_own(1, 0, S)
-        gather(1, 0, mid)
+        gather(1, 0, mid, 8704)
         turn_partner(1, 0, mid)
         turn_own(2, 0, S)
-        gather(1, mid, S)
+        gather(1, mid, S, 9728)
         turn_partner(1, mid, S)
         turn_own(3, 0, S)
         for c0, c1 in [(0, mid), (mid, S)]:

@@ -29,7 +29,6 @@ BLOCKS = S // P
 TILES = H // P
 HALF = H // 2
 LINE = 4
-EXTRA = 64
 LAST_AT = (1024, 8192)
 TINY = 2.0**-60
 HUGE = 2.0**120
@@ -159,8 +158,8 @@ def tile_picked_mixup_gelu_e_kernel(
         weave_pair(1, 0, 0, S)
         pick(6, True)
         pick(7, False, 0, P)
-        pick(7, False, P, 2 * P + EXTRA)
-        pick(7, True, 2 * P + EXTRA, S)
+        pick(7, False, P, 2 * P)
+        pick(7, True, 2 * P, S)
 
         piece = P * PACK
         w_grouped = [sb("w_grouped%d" % t, [P, PASSES * piece], BF16) for t in range(TILES)]
@@ -364,7 +363,7 @@ def tile_picked_mixup_gelu_e_kernel(
         for b in range(BLOCKS):
             scale(True, b, 0, last)
         for b in range(BLOCKS):
-            scale(False, b, last, TILES)
+            scale(b == last, b, last, TILES)
         for b, dst in enumerate([apart[0][:, HALF:], bank(2)[:, :HALF], apart[1][:, HALF:], bank(3)[:, :HALF]]):
             turn_back(b, dst)
         for b in range(BLOCKS):

@@ -29,6 +29,7 @@ BLOCKS = S // P
 TILES = H // P
 HALF = H // 2
 LINE = 4
+X_LOADS = [(0, 2)] + [(n, n + 1) for n in range(2, PASSES * PACK)]
 LAST_AT = (1024, 8192)
 TINY = 2.0**-60
 HUGE = 2.0**120
@@ -54,17 +55,18 @@ def tile_picked_mixup_gelu_e_kernel(
         offs_sb = keep.tile([P, S // 16], U16, name="offs_sb")
         pos_sb = keep.tile([P, S // 16], U16, name="pos_sb")
 
-        x_rows = xT.rearrange("(g p j) c -> g j p c", p=P, j=PACK)
+        x_rows = xT.rearrange("(g p j) c -> g p j c", p=P, j=PACK)
         w_rows = w1.rearrange("(g p j) c -> g p j c", p=P, j=PACK)
         loaded_rows = sb("loaded_rows", [2 * BLOCKS, P], F32)
+        nc.scalar.dma_start(out=loaded_rows[0:BLOCKS, :], in_=lam[0:1, :].rearrange("o (b j) -> (o b) j", j=P))
+        nc.scalar.dma_start(out=loaded_rows[BLOCKS:, :], in_=mu[0:1, :].rearrange("o (b j) -> (o b) j", j=P))
         x_raw = []
-        for n in range(PASSES * PACK):
-            x_raw.append(sb("x_raw%d" % n, [P, T], F32))
-            nc.sync.dma_start(out=x_raw[n][:], in_=x_rows[n // PACK, n % PACK])
-            if n == 0:
+        for n0, n1 in X_LOADS:
+            rows = sb("x_raw%d" % n0, [P, n1 - n0, T], F32)
+            nc.sync.dma_start(out=rows[:], in_=x_rows[n0 // PACK, :, n0 % PACK : (n1 - 1) % PACK + 1])
+            x_raw.extend(rows[:, n - n0] for n in range(n0, n1))
+            if n0 == 0:
                 nc.sync.dma_start(offs_sb[:], offs)
-                nc.sync.dma_start(out=loaded_rows[0:BLOCKS, :], in_=lam[0:1, :].rearrange("o (b j) -> (o b) j", j=P))
-                nc.sync.dma_start(out=loaded_rows[BLOCKS:, :], in_=mu[0:1, :].rearrange("o (b j) -> (o b) j", j=P))
         w_raw = {}
         w_both = {2: sb("w_both2", [P, PASSES, PACK, P], F32)}
         for t in range(TILES):
@@ -102,8 +104,8 @@ def tile_picked_mixup_gelu_e_kernel(
         share_bank = bank(6)
         nc.tensor.transpose(share_bank[:, 0:P], share_rows[:], ident[:])
         lam_cols = sb("lam_cols", [P, BLOCKS], F32)
-        planes = [sb("planes%d" % g, [P, PACK, S], BF16) for g in range(PASSES)]
-        inverse = planes[0][:, PACK - 1, : 2 * BLOCKS].bitcast(F32)
+        planes = [sb("planes%d" % g, [P, PACK, S], dtype) for g, dtype in enumerate((F32, BF16))]
+        inverse = planes[0][:, PACK - 1, :BLOCKS]
         ratio_cols = sb("ratio_cols", [P, BLOCKS], F32)
         nc.vector.reciprocal(out=inverse, in_=share_bank[:, 0:BLOCKS])
         nc.vector.tensor_copy(out=lam_cols[:], in_=share_bank[:, 0:BLOCKS])
@@ -123,7 +125,7 @@ def tile_picked_mixup_gelu_e_kernel(
                 nc.vector.tensor_copy(out=dst, in_=src)
 
         def pick(n, on_scalar, c0=0, c1=S):
-            move(on_scalar, planes[n // PACK][:, n % PACK, c0:c1], x_raw[n][:].indirect(offs_sb[:, c0 // 16 : c1 // 16]))
+            move(on_scalar, planes[n // PACK][:, n % PACK, c0:c1], x_raw[n].indirect(offs_sb[:, c0 // 16 : c1 // 16]))
 
         def weave(on_scalar, grouped, rows):
             move(
@@ -363,7 +365,7 @@ def tile_picked_mixup_gelu_e_kernel(
         for b in range(BLOCKS):
             scale(True, b, 0, last)
         for b in range(BLOCKS):
-            scale(b == last, b, last, TILES)
+            scale(False, b, last, TILES)
         for b, dst in enumerate([apart[0][:, HALF:], bank(2)[:, :HALF], apart[1][:, HALF:], bank(3)[:, :HALF]]):
             turn_back(b, dst)
         for b in range(BLOCKS):

@@ -29,7 +29,7 @@ BLOCKS = S // P
 TILES = H // P
 HALF = H // 2
 LINE = 4
-X_LOADS = [(0, 2)] + [(n, n + 1) for n in range(2, PASSES * PACK)]
+X_LOADS = [(0, 2), (2, 4)] + [(n, n + 1) for n in range(PACK, PASSES * PACK)]
 LAST_AT = (1024, 8192)
 TINY = 2.0**-60
 HUGE = 2.0**120
@@ -149,10 +149,8 @@ def tile_picked_mixup_gelu_e_kernel(
         def quantise_x(g, c0, c1):
             quantise(x_words[g][:, c0:c1], x_bytes[g][:, c0:c1], x_grouped[g][:, c0 * PACK : c1 * PACK])
 
-        for n in range(PACK - 1):
+        for n in range(PACK):
             pick(n, n % 2 == 0)
-        pick(3, False, 0, S // 2)
-        pick(3, True, S // 2, S)
         weave(False, x_grouped[0][:], planes[0][:])
         pick(4, True)
         quantise_x(0, 0, S)
@@ -355,10 +353,10 @@ def tile_picked_mixup_gelu_e_kernel(
                     stop=True,
                 )
 
-        def store(b, copy):
+        def store(b, copy, queue):
             staged = sb("staged%d" % b, [P, N], F32)
             copy(out=staged[:], in_=results[b][:, :N])
-            nc.sync.dma_start(
+            queue.dma_start(
                 out=out_rows[:, :, b * P : (b + 1) * P], in_=staged[:].rearrange("p (a j) -> p a j", j=P)
             )
 
@@ -373,4 +371,4 @@ def tile_picked_mixup_gelu_e_kernel(
         for b in range(BLOCKS):
             finish(b)
         for b in range(BLOCKS):
-            store(b, nc.vector.tensor_copy if b % 2 else nc.scalar.copy)
+            store(b, *((nc.vector.tensor_copy, nc.sync) if b % 2 else (nc.scalar.copy, nc.scalar)))

from contextlib import ExitStack

import concourse.mybir as mybir
from concourse.masks import make_identity

K, T, S, H, N = 1024, 1024, 512, 512, 256
FLOPS = 2 * K * H * S + 2 * H * N * S

F32 = mybir.dt.float32
BF16 = mybir.dt.bfloat16
I32 = mybir.dt.int32
U32 = mybir.dt.uint32
U16 = mybir.dt.uint16
U8 = mybir.dt.uint8
FP8X4 = mybir.dt.float8_e4m3fn_x4
FP4X4 = mybir.dt.float4_e2m1fn_x4
COPY = mybir.ActivationFunctionType.Copy
GELU = mybir.ActivationFunctionType.Gelu_apprx_tanh
MULT = mybir.AluOpType.mult
ADD = mybir.AluOpType.add
IS_LE = mybir.AluOpType.is_le
MAX = mybir.AluOpType.max

P = 128
PACK = 4
PASSES = K // (P * PACK)
PAIR = 2
BLOCKS = S // P
TILES = H // P
HALF = H // 2
LINE = 4
X_LOADS = [(0, 2), (2, 4)] + [(n, n + 1) for n in range(PACK, PASSES * PACK)]
LAST_AT = (1024, 8192)
TINY = 2.0**-60
HUGE = 2.0**120


def tile_picked_mixup_gelu_e_kernel(
    tc, xT, w1, w2_words, w2_scales, lam, mu, offs, pos1, out
):
    nc = tc.nc
    with ExitStack() as ctx:
        keep = ctx.enter_context(tc.tile_pool(name="keep", bufs=1))
        shared = ctx.enter_context(tc.tile_pool(name="shared", bufs=1))
        psum = ctx.enter_context(tc.psum_pool(name="psum", bufs=1))

        def sb(name, shape, dtype, tag=None):
            if isinstance(tag, int):
                return shared.tile(shape, dtype, name=name, offset=tag, align_bytes=64)
            return keep.tile(shape, dtype, name=name, tag=tag or name, align_bytes=64)

        def bank(index):
            return psum.tile([P, S], F32, name="bank%d" % index)

        offs_sb = keep.tile([P, S // 16], U16, name="offs_sb")
        pos_sb = keep.tile([P, S // 16], U16, name="pos_sb")

        x_rows = xT.rearrange("(g p j) c -> g p j c", p=P, j=PACK)
        w_rows = w1.rearrange("(g p j) c -> g p j c", p=P, j=PACK)
        loaded_rows = sb("loaded_rows", [2 * BLOCKS, P], F32)
        nc.scalar.dma_start(out=loaded_rows[0:BLOCKS, :], in_=lam[0:1, :].rearrange("o (b j) -> (o b) j", j=P))
        nc.scalar.dma_start(out=loaded_rows[BLOCKS:, :], in_=mu[0:1, :].rearrange("o (b j) -> (o b) j", j=P))
        x_raw = []
        for n0, n1 in X_LOADS:
            rows = sb("x_raw%d" % n0, [P, n1 - n0, T], F32)
            nc.sync.dma_start(out=rows[:], in_=x_rows[n0 // PACK, :, n0 % PACK : (n1 - 1) % PACK + 1])
            x_raw.extend(rows[:, n - n0] for n in range(n0, n1))
            if n0 == 0:
                nc.sync.dma_start(offs_sb[:], offs)
        w_raw = {}
        w_both = {2: sb("w_both2", [P, PASSES, PACK, P], F32)}
        for t in range(TILES):
            for g in range(PASSES):
                w_raw[t, g] = w_both[t][:, g] if t in w_both else sb("w_raw%d%d" % (t, g), [P, PACK, P], F32, LAST_AT[g] if t == 3 else None)[:]
                nc.sync.dma_start(out=w_raw[t, g], in_=w_rows[g, :, :, t * P : (t + 1) * P])
            if t == 1:
                nc.sync.dma_start(pos_sb[:], pos1)
        w2_codes = sb("w2_codes", [P, 2 * N], U8)
        w2_bytes = sb("w2_bytes", [P, N], U8)
        nc.vector.memset(w2_bytes[:].bitcast(I32), 0)
        nc.sync.dma_start(out=w2_codes[:].bitcast(I32), in_=w2_words[0].bitcast(I32))
        for q in range(4):
            nc.sync.dma_start(
                out=w2_bytes[32 * q : 32 * q + 4, :].bitcast(I32),
                in_=w2_scales[0, 4 * q : 4 * q + 4, :].bitcast(I32),
            )

        ident = sb("ident", [P, P], F32)
        share_rows = sb("share_rows", [P, P], F32)
        zeros = sb("zeros", [P, 8], F32)
        warm = sb("warm", [P, 8], F32)
        nc.vector.memset(zeros[:], 0.0)
        nc.vector.memset(share_rows[:], 0.0)
        make_identity(nc, ident[:])
        nc.scalar.activation(out=warm[:], in_=zeros[:], func=GELU)

        floor = sb("floor", [2 * BLOCKS, P], F32)
        nc.vector.tensor_scalar(
            out=floor[:], in0=loaded_rows[:], scalar1=-TINY, scalar2=-HUGE, op0=IS_LE, op1=MULT
        )
        nc.vector.scalar_tensor_tensor(
            out=share_rows[0 : 2 * BLOCKS, :], in0=floor[:], scalar=TINY, in1=loaded_rows[:], op0=ADD, op1=MAX
        )
        share_bank = bank(6)
        nc.tensor.transpose(share_bank[:, 0:P], share_rows[:], ident[:])
        lam_cols = sb("lam_cols", [P, BLOCKS], F32)
        planes = [sb("planes%d" % g, [P, PACK, S], dtype) for g, dtype in enumerate((F32, BF16))]
        inverse = planes[0][:, PACK - 1, :BLOCKS]
        ratio_cols = sb("ratio_cols", [P, BLOCKS], F32)
        nc.vector.reciprocal(out=inverse, in_=share_bank[:, 0:BLOCKS])
        nc.vector.tensor_copy(out=lam_cols[:], in_=share_bank[:, 0:BLOCKS])
        nc.vector.tensor_tensor(out=ratio_cols[:], in0=share_bank[:, BLOCKS : 2 * BLOCKS], in1=inverse, op=MULT)
        ratio_bank = bank(7)
        for b in range(BLOCKS):
            nc.tensor.transpose(
                ratio_bank[:, b * P : (b + 1) * P], ratio_cols[:, b : b + 1].to_broadcast([P, P]), ident[:]
            )
        ratio = sb("ratio", [P, S], F32)
        nc.vector.tensor_copy(out=ratio[:], in_=ratio_bank[:])

        def move(on_scalar, dst, src):
            if on_scalar:
                nc.scalar.activation(out=dst, in_=src, func=COPY)
            else:
                nc.vector.tensor_copy(out=dst, in_=src)

        def pick(n, on_scalar, c0=0, c1=S):
            move(on_scalar, planes[n // PACK][:, n % PACK, c0:c1], x_raw[n].indirect(offs_sb[:, c0 // 16 : c1 // 16]))

        def weave(on_scalar, grouped, rows):
            move(
                on_scalar,
                grouped.rearrange("p (c i j) -> p c j i", i=LINE, j=PACK),
                rows.rearrange("p j (c i) -> p c j i", i=LINE),
            )

        def quantise(words, scale_bytes, values):
            nc.vector.quantize_mx(out=words.bitcast(FP8X4), scales=scale_bytes, in_=values)

        x_grouped = [sb("x_grouped%d" % g, [P, S * PACK], BF16) for g in range(PASSES)]
        x_words = {0: sb("x_words0", [P, S], U32)}
        x_bytes = [sb("x_bytes%d" % g, [P, S], U8) for g in range(PASSES)]

        def weave_pair(g, u, c0, c1):
            words = x_grouped[g][:, c0 * PACK : c1 * PACK].rearrange("p (c i u e) -> p u c e i", i=LINE, u=PACK // PAIR, e=PAIR)
            rows = planes[g][:, PAIR * u : PAIR * (u + 1), c0:c1].rearrange("p e (c i) -> p c e i", i=LINE)
            nc.vector.tensor_copy(out=words[:, u], in_=rows)

        def quantise_x(g, c0, c1):
            quantise(x_words[g][:, c0:c1], x_bytes[g][:, c0:c1], x_grouped[g][:, c0 * PACK : c1 * PACK])

        for n in range(PACK):
            pick(n, n % 2 == 0)
        weave(False, x_grouped[0][:], planes[0][:])
        pick(4, True)
        quantise_x(0, 0, S)
        pick(5, True)
        weave_pair(1, 0, 0, S)
        pick(6, True)
        pick(7, False, 0, P)
        pick(7, False, P, 2 * P)
        pick(7, True, 2 * P, S)

        piece = P * PACK
        w_grouped = [sb("w_grouped%d" % t, [P, PASSES * piece], BF16) for t in range(TILES)]
        w_words = {}
        w_bytes = {}

        def round_w(on_scalar, t, g):
            weave(on_scalar, w_grouped[t][:, g * piece : (g + 1) * piece], w_raw[t, g])

        def quantise_w(t, g0, g1):
            words = sb("w_words%d%d" % (t, g0), [P, (g1 - g0) * P], U32)
            scale_bytes = sb("w_bytes%d%d" % (t, g0), [P, (g1 - g0) * P], U8)
            quantise(words[:], scale_bytes[:], w_grouped[t][:, g0 * piece : g1 * piece])
            for g in range(g0, g1):
                w_words[t, g] = words[:, (g - g0) * P : (g - g0 + 1) * P]
                w_bytes[t, g] = scale_bytes[:, (g - g0) * P : (g - g0 + 1) * P]

        acc = {}

        def multiply(dst, t, g, c0, c1, start, stop):
            nc.tensor.matmul_mx(
                out=dst[:, c0:c1],
                lhsT=w_words[t, g].bitcast(FP8X4),
                lhsT_scale=w_bytes[t, g],
                rhs=x_words[g][:, c0:c1].bitcast(FP8X4),
                rhs_scale=x_bytes[g][:, c0:c1],
                start=start,
                stop=stop,
            )

        def product(t):
            acc[t] = bank(t)
            for g in range(PASSES):
                multiply(acc[t], t, g, 0, S, g == 0, g == PASSES - 1)

        h = {}
        fetched = {}

        def gelu(t, tag=None):
            h[t] = sb("h%d" % t, [P, S], F32, tag)
            nc.scalar.activation(out=h[t][:], in_=acc[t][:], func=GELU)

        def fetch(t, c0, c1, tag=None):
            fetched[t, c0] = sb("fetched%d_%d" % (t, c0), [P, c1 - c0], F32, tag)
            move(True, fetched[t, c0][:], h[t][:].indirect(pos_sb[:, c0 // 16 : c1 // 16]))

        mid = S // 2
        for t, g in [(0, 0), (0, 1), (1, 0), (1, 1)]:
            round_w(True, t, g)
        for c0, c1 in [(0, P), (P, mid), (mid, S)]:
            weave_pair(1, 1, c0, c1)
        quantise_w(0, 0, 1)
        quantise_w(0, 1, 2)
        x_words[1] = sb("x_words1", [P, S], U32, "w_raw01")
        pieces = [(bank(0), 0, mid), (bank(4), mid, mid + P), (bank(5), mid + P, S)]
        for half, c0, c1 in pieces:
            quantise_x(1, c0, c1)
        h[0] = sb("h0", [P, S], F32, "w_raw11")
        for g in range(PASSES):
            for half, c0, c1 in pieces:
                multiply(half, 0, g, c0, c1, g == 0, g == PASSES - 1)
        for half, c0, c1 in pieces:
            nc.scalar.activation(out=h[0][:, c0:c1], in_=half[:, c0:c1], func=GELU)
        quantise_w(1, 0, PASSES)
        product(1)
        nc.vector.tensor_copy(
            out=w_grouped[2][:].rearrange("p (g c i j) -> p g c j i", g=PASSES, i=LINE, j=PACK),
            in_=w_both[2][:].rearrange("p g j (c i) -> p g c j i", i=LINE),
        )
        quantise_w(2, 0, PASSES)
        product(2)
        round_w(True, 3, 0)
        quantise_w(3, 0, 1)
        acc[3] = bank(3)
        multiply(acc[3], 3, 0, 0, S, True, False)
        gelu(1, 0)
        round_w(True, 3, 1)
        gelu(2, 6656)

        partner = {}

        def place(t, c0, c1, tag):
            part = sb("term%d_%d" % (t, c0), [P, c1 - c0], F32, tag)[:]
            for b in range(c0 // P, c1 // P):
                partner[t, b] = part[:, b * P - c0 : (b + 1) * P - c0]
            return part

        def gather(t, c0, c1, tag=None):
            nc.vector.tensor_tensor(
                out=place(t, c0, c1, tag),
                in0=h[t][:].indirect(pos_sb[:, c0 // 16 : c1 // 16]),
                in1=ratio[:, c0:c1],
                op=MULT,
            )

        def weigh(t, c0, c1):
            nc.vector.tensor_tensor(out=place(t, c0, c1, None), in0=fetched[t, c0][:], in1=ratio[:, c0:c1], op=MULT)

        last = TILES - 1
        early = [bank(index) for index in (5, 6, 7, 0)]
        apart = [bank(index) for index in (4, 1)]
        left = {}

        def home(t, b):
            if t < last:
                return ("early", b), early[b][:, t * P : (t + 1) * P], 2 * last
            return ("apart", b // 2), apart[b // 2][:, (b % 2) * P : (b % 2 + 1) * P], 4

        def turn(t, b, src):
            group, dst, size = home(t, b)
            left[group] = left.get(group, size) - 1
            nc.tensor.matmul(
                dst, lhsT=src, rhs=ident[:], is_transpose=True, start=(left[group] == size - 1), stop=(left[group] == 0)
            )

        def turn_partner(t, c0, c1):
            for b in range(c0 // P, c1 // P):
                turn(t, b, partner[t, b])

        def turn_own(t, c0, c1):
            for b in range(c0 // P, c1 // P):
                turn(t, b, h[t][:, b * P : (b + 1) * P])

        turned = [sb("turned%d" % b, [P, H], BF16) for b in range(BLOCKS)]

        def scale(on_scalar, b, t0, t1):
            dst = turned[b][:].rearrange("j (u l e) -> j u l e", u=PACK // PAIR, e=PAIR)[:, :, t0 * 32 : t1 * 32]
            src = early[b][:, : last * P] if t0 == 0 else home(last, b)[1]
            src = src.rearrange("j (l u e) -> j u l e", u=PACK // PAIR, e=PAIR)
            if on_scalar:
                nc.scalar.activation(out=dst, in_=src, func=COPY, scale=lam_cols[:, b : b + 1])
            else:
                nc.vector.tensor_scalar(out=dst, in0=src, scalar1=lam_cols[:, b : b + 1], scalar2=None, op0=MULT)

        back = {}

        def turn_back(b, dst):
            back[b] = dst
            words = turned[b][:].bitcast(F32)
            for u in range(PACK // PAIR):
                nc.tensor.transpose(dst[:, u * P : (u + 1) * P], words[:, u * P : (u + 1) * P], ident[:])

        turn_own(0, 0, S)
        gather(0, 0, mid, "w_both2")
        turn_partner(0, 0, mid)
        quantise_w(3, 1, PASSES)
        multiply(acc[3], 3, 1, 0, S, False, True)
        gelu(3)
        fetch(3, 0, mid)
        fetch(3, mid, S)
        gather(0, mid, S, 2048)
        turn_partner(0, mid, S)
        turn_own(1, 0, S)
        gather(1, 0, mid, 8704)
        turn_partner(1, 0, mid)
        turn_own(2, 0, S)
        gather(1, mid, S, 9728)
        turn_partner(1, mid, S)
        turn_own(3, 0, S)
        for c0, c1 in [(0, mid), (mid, S)]:
            gather(2, c0, c1)
            turn_partner(2, c0, c1)
        for c0, c1 in [(0, mid), (mid, S)]:
            weigh(3, c0, c1)
            turn_partner(3, c0, c1)

        out_rows = out.rearrange("(a m) j -> m a j", m=P)
        results = {}
        z = {}

        def weave_z(b, copy):
            z[b] = sb("z%d" % b, [P, P * PACK], BF16)
            copy(
                out=z[b][:].bitcast(F32).rearrange("p (j u) -> p j u", u=PACK // PAIR),
                in_=back[b].rearrange("p (u j) -> p j u", u=PACK // PAIR),
            )

        def finish(b):
            z_words = sb("z_words%d" % b, [P, P], U32)
            z_bytes = sb("z_bytes%d" % b, [P, P], U8)
            quantise(z_words[:], z_bytes[:], z[b][:])
            results[b] = bank([5, 6, 7, 0][b])
            for a in range(N // P):
                nc.tensor.matmul_mx(
                    out=results[b][:, a * P : (a + 1) * P],
                    lhsT=w2_codes[:, 2 * a * P : 2 * (a + 1) * P].bitcast(FP4X4),
                    lhsT_scale=w2_bytes[:, a * P : (a + 1) * P],
                    rhs=z_words[:].bitcast(FP8X4),
                    rhs_scale=z_bytes[:],
                    start=True,
                    stop=True,
                )

        def store(b, copy, queue):
            staged = sb("staged%d" % b, [P, N], F32)
            copy(out=staged[:], in_=results[b][:, :N])
            queue.dma_start(
                out=out_rows[:, :, b * P : (b + 1) * P], in_=staged[:].rearrange("p (a j) -> p a j", j=P)
            )

        for b in range(BLOCKS):
            scale(True, b, 0, last)
        for b in range(BLOCKS):
            scale(False, b, last, TILES)
        for b, dst in enumerate([apart[0][:, HALF:], bank(2)[:, :HALF], apart[1][:, HALF:], bank(3)[:, :HALF]]):
            turn_back(b, dst)
        for b in range(BLOCKS):
            weave_z(b, nc.scalar.copy if b % 2 else nc.vector.tensor_copy)
        for b in range(BLOCKS):
            finish(b)
        for b in range(BLOCKS):
            store(b, *((nc.vector.tensor_copy, nc.sync) if b % 2 else (nc.scalar.copy, nc.scalar)))
